import numpy as np
import ml_dtypes


def mxq(x, axis, fmt="e4m3"):
    dtype, down = {"e4m3": (ml_dtypes.float8_e4m3fn, 7), "e5m2": (ml_dtypes.float8_e5m2, 14)}[fmt]
    v = np.moveaxis(np.asarray(x, np.float32).astype(ml_dtypes.bfloat16).astype(np.float64), axis, -1)
    blocks = v.reshape(v.shape[:-1] + (-1, 32))
    amax = np.abs(blocks).max(-1, keepdims=True)
    byte = np.maximum(np.where(amax > 0, np.frexp(amax)[1] - 1 + 127, 0) - down, 1)
    scale = np.exp2(byte - 127.0)
    codes = (blocks / scale).astype(np.float32).astype(dtype).astype(np.float64)
    return np.moveaxis((codes * scale).reshape(v.shape), -1, axis)


WIDE = False


def mx_kscale(k):
    if not WIDE:
        return np.ones(k)
    levels = np.array([10, -10, 5, -5, 0])
    if k % 512:
        return np.exp2(np.random.permutation(np.resize(levels, k // 32))).repeat(32)
    a = np.empty((k // 512, 16))
    for p in range(k // 512):
        a[p, :8] = np.random.permutation(np.resize(levels, 8))
        for g in range(8):
            far = levels[np.abs(levels - a[p, g]) >= 10]
            a[p, g + 8] = far[np.random.randint(len(far))]
    return np.exp2(a.ravel()).repeat(32)


def f64(x):
    return np.asarray(x).astype(np.float64)


def striped8(idx):
    return np.asarray(idx).reshape(8, -1, 16).transpose(0, 2, 1).reshape(128, -1).astype(np.uint16)


def unstriped8(offs):
    return offs.reshape(8, 16, -1).transpose(0, 2, 1).reshape(8, -1).astype(np.int64)


def pick8(x, idx, run):
    r = np.arange(len(x))
    return x[r[:, None], idx[r % (8 * run) // run]]


D, C, Q, I, M = 512, 1024, 512, 512, 128


def setup_inputs():
    n = np.random.standard_normal
    idx = np.stack([np.random.randint(0, C, I) for _ in range(8)])
    fd = mx_kscale(D)
    fq = mx_kscale(Q)
    return {
        "query": (n((D, Q)) * (np.arange(D)[:, None] // 64 == np.arange(Q) // 64) * 0.125 * fd[:, None]).astype(np.float32),
        "book": (n((D, C)) / fd[:, None]).astype(np.float32),
        "fac": (np.random.uniform(0.5, 2.0, (Q, 1)) * fq[:, None]).astype(np.float32),
        "pat": (n((Q, M)) * 1 / np.sqrt(Q) / fq[:, None]).astype(np.float32),
        "offs": striped8(idx),
    }


def reference(query, book, fac, pat, offs):
    idx = unstriped8(offs)
    queryq = mxq(f64(query), 0, "e4m3")
    bookq = mxq(f64(book), 0, "e4m3")
    a = queryq.T @ bookq
    b = pick8(a, idx, 64) * f64(fac)
    patq = mxq(f64(pat), 0, "e4m3")
    bq = mxq(b, 0, "e4m3")
    y = patq.T @ bq
    return y

@@ -1,0 +1,187 @@
+from contextlib import ExitStack
+
+import concourse.mybir as mybir
+
+D, C, Q, I, M = 512, 1024, 512, 512, 128
+FLOPS = 2 * D * Q * C + 2 * Q * M * I
+BYTES = 4 * (4 * 128 * 128 + D * C + Q + Q * M + M * I) + 2 * 128 * (I // 16)
+
+F32 = mybir.dt.float32
+BF16 = mybir.dt.bfloat16
+U32 = mybir.dt.uint32
+U16 = mybir.dt.uint16
+U8 = mybir.dt.uint8
+FP8X4 = mybir.dt.float8_e4m3fn_x4
+MULT = mybir.AluOpType.mult
+
+P = 128
+PACK = 4
+QUAD = 32
+BOOK_LOADS = (256, 256, 256, 128, 128)
+UNIT = 128
+SLOT_PIECES = (256, 128, 128)
+
+
+def interleave(engine_copy, grouped, planes):
+    engine_copy(
+        grouped.rearrange("p (c i) j -> p c j i", i=4),
+        planes.rearrange("p j (c i) -> p c j i", i=4),
+    )
+
+
+def quantise(nc, pool, grouped, width, name):
+    codes = pool.tile([P, width], U32, name=name + "_codes", align_bytes=64)
+    scales = pool.tile([P, width], U8, name=name + "_scales", align_bytes=64)
+    nc.vector.quantize_mx(out=codes[:].bitcast(FP8X4), scales=scales[:], in_=grouped)
+    return codes, scales
+
+
+def tile_attend_adcheads_kernel(tc, query, book, fac, pat, offs, out):
+    nc = tc.nc
+    with ExitStack() as ctx:
+        keep = ctx.enter_context(tc.tile_pool(name="keep", bufs=1))
+        psum = ctx.enter_context(tc.psum_pool(name="psum", bufs=1))
+
+        q_raw = keep.tile([P, PACK, P], F32)
+        for quad in (0, 2, 1, 3):
+            queue = nc.sync if quad < 2 else nc.scalar
+            rows = slice(P * quad, P * (quad + 1))
+            queue.dma_start(
+                q_raw[QUAD * quad : QUAD * (quad + 1), :, :],
+                query[rows, rows].rearrange("(p j) c -> p j c", j=PACK),
+            )
+        fac_sb = keep.tile([P, PACK], F32)
+        nc.scalar.dma_start(fac_sb[:], fac.rearrange("(p t) o -> p (t o)", t=PACK))
+
+        book_rows = book.rearrange("(p j) c -> p j c", j=PACK)
+        book_raw = []
+        c0 = 0
+        for n, width in enumerate(BOOK_LOADS):
+            raw = keep.tile([P, PACK, width], F32, name="book_raw%d" % n)
+            nc.sync.dma_start(raw[:], book_rows[:, :, c0 : c0 + width])
+            book_raw.append(raw)
+            c0 = c0 + width
+        offsets = keep.tile([P, I // 16], U16)
+        nc.sync.dma_start(offsets[:], offs)
+        pat_raw = keep.tile([P, PACK, M], F32)
+        nc.sync.dma_start(pat_raw[:], pat.rearrange("(p j) m -> p j m", j=PACK))
+
+        q_grouped = keep.tile([P, PACK, P, PACK], BF16, align_bytes=64)
+        nc.vector.memset(q_grouped[:], 0.0)
+        for quad in (0, 2, 1, 3):
+            parts = slice(QUAD * quad, QUAD * (quad + 1))
+            copy = nc.scalar.copy if quad == 2 else nc.vector.tensor_copy
+            copy(
+                q_grouped[parts, :, parts, :].rearrange("p t m j -> p m j t"),
+                q_raw[parts, :, :].rearrange("p j (m t) -> p m j t", t=PACK),
+            )
+        q_codes, q_scales = quantise(nc, keep, q_grouped[:].rearrange("p t m j -> p (t m j)"), Q, "q")
+
+        scores = [keep.tile([P, C], F32, name="scores%d" % t) for t in range(PACK)]
+        book_codes = keep.tile([P, C], U32, align_bytes=64)
+        book_scales = keep.tile([P, C], U8, align_bytes=64)
+        load_starts = [sum(BOOK_LOADS[:n]) for n in range(len(BOOK_LOADS))]
+        on_scalar = (1, 6)
+        for n, width in enumerate(BOOK_LOADS):
+            units = []
+            for c0 in range(0, width, UNIT):
+                unit = (load_starts[n] + c0) // UNIT
+                grouped = keep.tile([P, UNIT, PACK], BF16, name="book_grouped%d" % unit, align_bytes=64)
+                copy = nc.scalar.copy if unit in on_scalar else nc.vector.tensor_copy
+                interleave(copy, grouped[:], book_raw[n][:, :, c0 : c0 + UNIT])
+                units.append((unit, grouped))
+            for unit, grouped in units:
+                cols = slice(UNIT * unit, UNIT * (unit + 1))
+                nc.vector.quantize_mx(
+                    out=book_codes[:, cols].bitcast(FP8X4),
+                    scales=book_scales[:, cols],
+                    in_=grouped[:].rearrange("p c j -> p (c j)"),
+                )
+
+        sums = {}
+
+        def score(n, planes, bank):
+            width = BOOK_LOADS[n]
+            entries = slice(load_starts[n], load_starts[n] + width)
+            acc = psum.tile([P, len(planes), width], F32, name="acc%d_%d" % (n, planes[0]), tag="bank%d" % bank)
+            for u, t in enumerate(planes):
+                cols = slice(P * t, P * (t + 1))
+                nc.tensor.matmul_mx(
+                    out=acc[:, u, :],
+                    lhsT=q_codes[:, cols].bitcast(FP8X4),
+                    lhsT_scale=q_scales[:, cols],
+                    rhs=book_codes[:, entries].bitcast(FP8X4),
+                    rhs_scale=book_scales[:, entries],
+                    start=True,
+                    stop=True,
+                )
+                sums[n, t] = acc[:, u, :]
+
+        def drain(n, t):
+            copy = nc.vector.tensor_copy if (n, t) == (4, 0) else nc.scalar.copy
+            copy(scores[t][:, load_starts[n] : load_starts[n] + BOOK_LOADS[n]], sums[n, t])
+
+        for n in range(3):
+            score(n, (0, 1), 2 * n)
+            score(n, (2, 3), 2 * n + 1)
+        score(3, (0, 1, 2, 3), 6)
+        score(4, (0,), 7)
+        drain(0, 0)
+        drain(0, 1)
+        score(4, (1, 2, 3), 0)
+
+        pat_grouped = keep.tile([P, M, PACK], BF16, align_bytes=64)
+        interleave(nc.vector.tensor_copy, pat_grouped[:], pat_raw[:])
+        for t in range(PACK):
+            for n in range(len(BOOK_LOADS)):
+                if n > 0 or t > 1:
+                    drain(n, t)
+        pat_codes, pat_scales = quantise(nc, keep, pat_grouped[:].rearrange("p m j -> p (m j)"), M, "pat")
+
+        widest = max(SLOT_PIECES)
+        fac_wide = keep.tile([P, PACK, widest], F32)
+        for t in range(PACK - 1):
+            nc.scalar.copy(fac_wide[:, t, :], fac_sb[:, t : t + 1].to_broadcast([P, widest]))
+        nc.scalar.copy(fac_wide[:, 3, 0:128], fac_sb[:, 3:4].to_broadcast([P, 128]))
+        fac_last = keep.tile([P, widest], F32, tag="later")
+        nc.scalar.copy(fac_last[:], fac_sb[:, 3:4].to_broadcast([P, widest]))
+
+        starts = [sum(SLOT_PIECES[:n]) for n in range(len(SLOT_PIECES))]
+
+        def look_up(planes, n, t, factors):
+            width = SLOT_PIECES[n]
+            piece = offsets[:, starts[n] // 16 : (starts[n] + width) // 16]
+            nc.vector.tensor_tensor(planes[:, t, :], scores[t][:].indirect(piece), factors, MULT)
+
+        first = keep.tile([P, PACK, 256], F32, tag="first", align_bytes=64)
+        for t in range(PACK):
+            look_up(first[:], 0, t, fac_wide[:, t, :] if t < 3 else fac_last[:])
+        later = keep.tile([P, 2, PACK, 128], F32, tag="later")
+        for n in (1, 2):
+            for t in range(PACK):
+                look_up(later[:, n - 1, :, :], n, t, fac_wide[:, t, 0:128])
+        looked = [first[:], later[:, 0, :, :], later[:, 1, :, :]]
+
+        s0 = 0
+        for n, width in enumerate(SLOT_PIECES):
+            last = n == len(SLOT_PIECES) - 1
+            grouped = keep.tile([P, width, PACK], BF16, name="b_grouped%d" % n, tag="first" if last else "b_grouped%d" % n, align_bytes=64)
+            interleave(nc.vector.tensor_copy if last else nc.scalar.copy, grouped[:], looked[n])
+            codes, scales = quantise(nc, keep, grouped[:].rearrange("p c j -> p (c j)"), width, "b%d" % n)
+            acc = psum.tile([P, width], F32, name="acc_out", tag="bank%d" % (7, 2, 4)[n])
+            nc.tensor.matmul_mx(
+                out=acc[:],
+                lhsT=pat_codes[:].bitcast(FP8X4),
+                lhsT_scale=pat_scales[:],
+                rhs=codes[:].bitcast(FP8X4),
+                rhs_scale=scales[:],
+                start=True,
+                stop=True,
+            )
+            result = keep.tile([P, width], F32, name="result%d" % n)
+            if last:
+                nc.vector.tensor_copy(result[:], acc[:])
+            else:
+                nc.scalar.copy(result[:], acc[:])
+            nc.sync.dma_start(out[:, s0 : s0 + width], result[:])
+            s0 = s0 + width

@@ -17,9 +17,11 @@ MULT = mybir.AluOpType.mult
 P = 128
 PACK = 4
 QUAD = 32
-BOOK_LOADS = (256, 256, 256, 128, 128)
 UNIT = 128
-SLOT_PIECES = (256, 128, 128)
+BANK = 512
+BOOK_LOADS = (128, 256, 256, 256, 128)
+PIECE = 128
+PIECES = I // PIECE
 
 
 def interleave(engine_copy, grouped, planes):
@@ -29,159 +31,174 @@ def interleave(engine_copy, grouped, planes):
     )
 
 
-def quantise(nc, pool, grouped, width, name):
-    codes = pool.tile([P, width], U32, name=name + "_codes", align_bytes=64)
-    scales = pool.tile([P, width], U8, name=name + "_scales", align_bytes=64)
-    nc.vector.quantize_mx(out=codes[:].bitcast(FP8X4), scales=scales[:], in_=grouped)
-    return codes, scales
-
-
 def tile_attend_adcheads_kernel(tc, query, book, fac, pat, offs, out):
     nc = tc.nc
     with ExitStack() as ctx:
         keep = ctx.enter_context(tc.tile_pool(name="keep", bufs=1))
         psum = ctx.enter_context(tc.psum_pool(name="psum", bufs=1))
 
+        def quantise(codes, scales, grouped):
+            nc.vector.quantize_mx(out=codes.bitcast(FP8X4), scales=scales, in_=grouped.rearrange("p c j -> p (c j)"))
+
+        def product(acc, lhs, lhs_cols, rhs, rhs_cols):
+            nc.tensor.matmul_mx(
+                out=acc,
+                lhsT=lhs[0][:, lhs_cols].bitcast(FP8X4),
+                lhsT_scale=lhs[1][:, lhs_cols],
+                rhs=rhs[0][:, rhs_cols].bitcast(FP8X4),
+                rhs_scale=rhs[1][:, rhs_cols],
+                start=True,
+                stop=True,
+            )
+
+        fac_sb = keep.tile([P, PACK], F32)
+        nc.scalar.dma_start(fac_sb[:], fac.rearrange("(p t) o -> p (t o)", t=PACK))
         q_raw = keep.tile([P, PACK, P], F32)
-        for quad in (0, 2, 1, 3):
-            queue = nc.sync if quad < 2 else nc.scalar
+        for quad in (0, 2, 3, 1):
+            queue = nc.scalar if quad == 2 else nc.sync
             rows = slice(P * quad, P * (quad + 1))
             queue.dma_start(
                 q_raw[QUAD * quad : QUAD * (quad + 1), :, :],
                 query[rows, rows].rearrange("(p j) c -> p j c", j=PACK),
             )
-        fac_sb = keep.tile([P, PACK], F32)
-        nc.scalar.dma_start(fac_sb[:], fac.rearrange("(p t) o -> p (t o)", t=PACK))
-
         book_rows = book.rearrange("(p j) c -> p j c", j=PACK)
         book_raw = []
         c0 = 0
         for n, width in enumerate(BOOK_LOADS):
-            raw = keep.tile([P, PACK, width], F32, name="book_raw%d" % n)
+            raw = keep.tile([P, PACK, width], F32, name="book_raw%d" % n, tag="book_raw%d" % n)
             nc.sync.dma_start(raw[:], book_rows[:, :, c0 : c0 + width])
             book_raw.append(raw)
             c0 = c0 + width
-        offsets = keep.tile([P, I // 16], U16)
-        nc.sync.dma_start(offsets[:], offs)
         pat_raw = keep.tile([P, PACK, M], F32)
         nc.sync.dma_start(pat_raw[:], pat.rearrange("(p j) m -> p j m", j=PACK))
+        offsets = keep.tile([P, I // 16], U16)
+        nc.sync.dma_start(offsets[:], offs)
+
+        fac_late = keep.tile([P, 2, PIECE], F32)
+        nc.scalar.copy(fac_late[:], fac_sb[:, 2:4].unsqueeze(2).to_broadcast([P, 2, PIECE]))
 
         q_grouped = keep.tile([P, PACK, P, PACK], BF16, align_bytes=64)
         nc.vector.memset(q_grouped[:], 0.0)
-        for quad in (0, 2, 1, 3):
+        for quad in (0, 2, 3, 1):
             parts = slice(QUAD * quad, QUAD * (quad + 1))
             copy = nc.scalar.copy if quad == 2 else nc.vector.tensor_copy
             copy(
                 q_grouped[parts, :, parts, :].rearrange("p t m j -> p m j t"),
                 q_raw[parts, :, :].rearrange("p j (m t) -> p m j t", t=PACK),
             )
-        q_codes, q_scales = quantise(nc, keep, q_grouped[:].rearrange("p t m j -> p (t m j)"), Q, "q")
+        q_codes = keep.tile([P, Q], U32, align_bytes=64)
+        q_scales = keep.tile([P, Q], U8, align_bytes=64)
+        quantise(q_codes[:], q_scales[:], q_grouped[:].rearrange("p t m j -> p (t m) j"))
+        q_mx = (q_codes, q_scales)
 
         scores = [keep.tile([P, C], F32, name="scores%d" % t) for t in range(PACK)]
         book_codes = keep.tile([P, C], U32, align_bytes=64)
         book_scales = keep.tile([P, C], U8, align_bytes=64)
-        load_starts = [sum(BOOK_LOADS[:n]) for n in range(len(BOOK_LOADS))]
-        on_scalar = (1, 6)
-        for n, width in enumerate(BOOK_LOADS):
-            units = []
-            for c0 in range(0, width, UNIT):
-                unit = (load_starts[n] + c0) // UNIT
-                grouped = keep.tile([P, UNIT, PACK], BF16, name="book_grouped%d" % unit, align_bytes=64)
-                copy = nc.scalar.copy if unit in on_scalar else nc.vector.tensor_copy
-                interleave(copy, grouped[:], book_raw[n][:, :, c0 : c0 + UNIT])
-                units.append((unit, grouped))
-            for unit, grouped in units:
-                cols = slice(UNIT * unit, UNIT * (unit + 1))
-                nc.vector.quantize_mx(
-                    out=book_codes[:, cols].bitcast(FP8X4),
-                    scales=book_scales[:, cols],
-                    in_=grouped[:].rearrange("p c j -> p (c j)"),
-                )
+        book_mx = (book_codes, book_scales)
 
-        sums = {}
+        starts = [sum(BOOK_LOADS[:n]) for n in range(len(BOOK_LOADS))]
+        book_grouped = [keep.tile([P, width, PACK], BF16, name="book_grouped%d" % n, align_bytes=64) for n, width in enumerate(BOOK_LOADS)]
 
-        def score(n, planes, bank):
+        def cast(n, c0, c1, copy):
+            interleave(copy, book_grouped[n][:, c0:c1, :], book_raw[n][:, :, c0:c1])
+
+        def quantise_book(n):
+            cols = slice(starts[n], starts[n] + BOOK_LOADS[n])
+            quantise(book_codes[:, cols], book_scales[:, cols], book_grouped[n][:])
+
+        outer = [psum.tile([P, BANK], F32, name="outer%d" % t, tag="bank%d" % t) for t in range(PACK)]
+        inner = [psum.tile([P, BANK], F32, name="inner%d" % t, tag="bank%d" % (PACK + t)) for t in range(PACK)]
+        places = [(outer, 0), (outer, 128), (inner, 0), (inner, 256), (outer, 384)]
+        places_first = [(outer, 0), (outer, 128), (inner, 0), (outer, 0), (inner, 256)]
+
+        def score(n, t):
+            banks, c0 = (places if t > 0 else places_first)[n]
             width = BOOK_LOADS[n]
-            entries = slice(load_starts[n], load_starts[n] + width)
-            acc = psum.tile([P, len(planes), width], F32, name="acc%d_%d" % (n, planes[0]), tag="bank%d" % bank)
-            for u, t in enumerate(planes):
-                cols = slice(P * t, P * (t + 1))
-                nc.tensor.matmul_mx(
-                    out=acc[:, u, :],
-                    lhsT=q_codes[:, cols].bitcast(FP8X4),
-                    lhsT_scale=q_scales[:, cols],
-                    rhs=book_codes[:, entries].bitcast(FP8X4),
-                    rhs_scale=book_scales[:, entries],
-                    start=True,
-                    stop=True,
-                )
-                sums[n, t] = acc[:, u, :]
+            product(banks[t][:, c0 : c0 + width], q_mx, slice(P * t, P * (t + 1)), book_mx, slice(starts[n], starts[n] + width))
 
-        def drain(n, t):
-            copy = nc.vector.tensor_copy if (n, t) == (4, 0) else nc.scalar.copy
-            copy(scores[t][:, load_starts[n] : load_starts[n] + BOOK_LOADS[n]], sums[n, t])
+        def drain(loads, t, copy):
+            banks, c0 = (places if t > 0 else places_first)[loads[0]]
+            width = sum(BOOK_LOADS[n] for n in loads)
+            copy(scores[t][:, starts[loads[0]] : starts[loads[0]] + width], banks[t][:, c0 : c0 + width])
 
-        for n in range(3):
-            score(n, (0, 1), 2 * n)
-            score(n, (2, 3), 2 * n + 1)
-        score(3, (0, 1, 2, 3), 6)
-        score(4, (0,), 7)
-        drain(0, 0)
-        drain(0, 1)
-        score(4, (1, 2, 3), 0)
+        cast(0, 0, UNIT, nc.scalar.copy)
+        quantise_book(0)
+        for t in range(PACK):
+            score(0, t)
+        fac_early = keep.tile([P, 2, 2 * PIECE], F32, tag="book_raw0")
+        nc.scalar.copy(fac_early[:], fac_sb[:, 0:2].unsqueeze(2).to_broadcast([P, 2, 2 * PIECE]))
+        fac_wide = (fac_early, fac_late)
+        cast(1, 0, 160, nc.vector.tensor_copy)
+        cast(1, 160, 256, nc.scalar.copy)
+        quantise_book(1)
+        for t in range(PACK):
+            score(1, t)
+        cast(2, 0, 160, nc.vector.tensor_copy)
+        cast(2, 160, 256, nc.scalar.copy)
+        quantise_book(2)
+        for t in range(PACK):
+            score(2, t)
+        cast(3, 0, 2 * UNIT, nc.vector.tensor_copy)
+        cast(4, 0, UNIT, nc.vector.tensor_copy)
+        quantise_book(3)
+        quantise_book(4)
+        drain((0, 1), 0, nc.scalar.copy)
+        drain((2,), 0, nc.scalar.copy)
+        score(3, 0)
+        score(4, 0)
+        drain((3,), 0, nc.scalar.copy)
+        drain((4,), 0, nc.vector.tensor_copy)
+        for t in (1, 2, 3):
+            drain((0, 1), t, nc.scalar.copy)
+        for t in (1, 2, 3):
+            score(3, t)
+            score(4, t)
 
         pat_grouped = keep.tile([P, M, PACK], BF16, align_bytes=64)
         interleave(nc.vector.tensor_copy, pat_grouped[:], pat_raw[:])
-        for t in range(PACK):
-            for n in range(len(BOOK_LOADS)):
-                if n > 0 or t > 1:
-                    drain(n, t)
-        pat_codes, pat_scales = quantise(nc, keep, pat_grouped[:].rearrange("p m j -> p (m j)"), M, "pat")
+        quantise(q_codes[:, 0:M], q_scales[:, 0:M], pat_grouped[:])
+        pat_mx = q_mx
 
-        widest = max(SLOT_PIECES)
-        fac_wide = keep.tile([P, PACK, widest], F32)
-        for t in range(PACK - 1):
-            nc.scalar.copy(fac_wide[:, t, :], fac_sb[:, t : t + 1].to_broadcast([P, widest]))
-        nc.scalar.copy(fac_wide[:, 3, 0:128], fac_sb[:, 3:4].to_broadcast([P, 128]))
-        fac_last = keep.tile([P, widest], F32, tag="later")
-        nc.scalar.copy(fac_last[:], fac_sb[:, 3:4].to_broadcast([P, widest]))
+        drain((2, 3), 1, nc.scalar.copy)
+        drain((4,), 1, nc.scalar.copy)
+        for t in (2, 3):
+            drain((2, 3), t, nc.scalar.copy)
+        for t in (2, 3):
+            drain((4,), t, nc.scalar.copy)
 
-        starts = [sum(SLOT_PIECES[:n]) for n in range(len(SLOT_PIECES))]
+        looked = [keep.tile([P, PACK, 2 * PIECE], F32, name="looked%d" % h, tag="looked%d" % h, align_bytes=64) for h in range(2)]
 
-        def look_up(planes, n, t, factors):
-            width = SLOT_PIECES[n]
-            piece = offsets[:, starts[n] // 16 : (starts[n] + width) // 16]
-            nc.vector.tensor_tensor(planes[:, t, :], scores[t][:].indirect(piece), factors, MULT)
-
-        first = keep.tile([P, PACK, 256], F32, tag="first", align_bytes=64)
-        for t in range(PACK):
-            look_up(first[:], 0, t, fac_wide[:, t, :] if t < 3 else fac_last[:])
-        later = keep.tile([P, 2, PACK, 128], F32, tag="later")
-        for n in (1, 2):
-            for t in range(PACK):
-                look_up(later[:, n - 1, :, :], n, t, fac_wide[:, t, 0:128])
-        looked = [first[:], later[:, 0, :, :], later[:, 1, :, :]]
-
-        s0 = 0
-        for n, width in enumerate(SLOT_PIECES):
-            last = n == len(SLOT_PIECES) - 1
-            grouped = keep.tile([P, width, PACK], BF16, name="b_grouped%d" % n, tag="first" if last else "b_grouped%d" % n, align_bytes=64)
-            interleave(nc.vector.tensor_copy if last else nc.scalar.copy, grouped[:], looked[n])
-            codes, scales = quantise(nc, keep, grouped[:].rearrange("p c j -> p (c j)"), width, "b%d" % n)
-            acc = psum.tile([P, width], F32, name="acc_out", tag="bank%d" % (7, 2, 4)[n])
-            nc.tensor.matmul_mx(
-                out=acc[:],
-                lhsT=pat_codes[:].bitcast(FP8X4),
-                lhsT_scale=pat_scales[:],
-                rhs=codes[:].bitcast(FP8X4),
-                rhs_scale=scales[:],
-                start=True,
-                stop=True,
+        def look_up(s0, width, t):
+            piece = offsets[:, s0 // 16 : (s0 + width) // 16]
+            c0 = s0 % (2 * PIECE)
+            nc.vector.tensor_tensor(
+                looked[s0 // (2 * PIECE)][:, t, c0 : c0 + width], scores[t][:].indirect(piece), fac_wide[t // 2][:, t % 2, :], MULT
             )
-            result = keep.tile([P, width], F32, name="result%d" % n)
-            if last:
-                nc.vector.tensor_copy(result[:], acc[:])
-            else:
-                nc.scalar.copy(result[:], acc[:])
+
+        for t in (0, 1):
+            for h in range(2):
+                look_up(2 * PIECE * h, 2 * PIECE, t)
+        for k in range(PIECES):
+            for t in (2, 3):
+                look_up(PIECE * k, PIECE, t)
+
+        def finish(name, grouped, s0, width, codes_tag, bank, copy):
+            codes = keep.tile([P, width], U32, name=name + "_codes", tag=codes_tag, align_bytes=64)
+            scales = keep.tile([P, width], U8, name=name + "_scales", align_bytes=64)
+            quantise(codes[:], scales[:], grouped)
+            acc = psum.tile([P, width], F32, name=name + "_acc", tag="bank%d" % bank)
+            product(acc[:], pat_mx, slice(0, M), (codes, scales), slice(0, width))
+            result = keep.tile([P, width], F32, name=name + "_result")
+            copy(result[:], acc[:])
             nc.sync.dma_start(out[:, s0 : s0 + width], result[:])
-            s0 = s0 + width
+
+        first = keep.tile([P, 2 * PIECE, PACK], BF16, align_bytes=64)
+        for k in (0, 1):
+            interleave(nc.scalar.copy, first[:, k * PIECE : (k + 1) * PIECE, :], looked[0][:, :, k * PIECE : (k + 1) * PIECE])
+        third = keep.tile([P, PIECE, PACK], BF16, align_bytes=64)
+        interleave(nc.scalar.copy, third[:], looked[1][:, :, 0:PIECE])
+        finish("first", first[:], 0, 2 * PIECE, "first_codes", 0, nc.scalar.copy)
+        fourth = keep.tile([P, PIECE, PACK], BF16, tag="looked0", align_bytes=64)
+        interleave(nc.vector.tensor_copy, fourth[:], looked[1][:, :, PIECE : 2 * PIECE])
+        finish("third", third[:], 2 * PIECE, PIECE, "third_codes", 1, nc.scalar.copy)
+        finish("fourth", fourth[:], 3 * PIECE, PIECE, "looked1", 4, nc.vector.tensor_copy)

@@ -19,7 +19,7 @@ PACK = 4
 QUAD = 32
 UNIT = 128
 BANK = 512
-BOOK_LOADS = (128, 256, 256, 256, 128)
+BOOK_LOADS = (384, 384, 256)
 PIECE = 128
 PIECES = I // PIECE
 
@@ -77,6 +77,8 @@ def tile_attend_adcheads_kernel(tc, query, book, fac, pat, offs, out):
         fac_late = keep.tile([P, 2, PIECE], F32)
         nc.scalar.copy(fac_late[:], fac_sb[:, 2:4].unsqueeze(2).to_broadcast([P, 2, PIECE]))
 
+        fac_early = keep.tile([P, 2, 2 * PIECE], F32)
+        fac_wide = (fac_early, fac_late)
         q_grouped = keep.tile([P, PACK, P, PACK], BF16, align_bytes=64)
         nc.vector.memset(q_grouped[:], 0.0)
         for quad in (0, 2, 3, 1):
@@ -86,6 +88,7 @@ def tile_attend_adcheads_kernel(tc, query, book, fac, pat, offs, out):
                 q_grouped[parts, :, parts, :].rearrange("p t m j -> p m j t"),
                 q_raw[parts, :, :].rearrange("p j (m t) -> p m j t", t=PACK),
             )
+        nc.scalar.copy(fac_early[:], fac_sb[:, 0:2].unsqueeze(2).to_broadcast([P, 2, 2 * PIECE]))
         q_codes = keep.tile([P, Q], U32, align_bytes=64)
         q_scales = keep.tile([P, Q], U8, align_bytes=64)
         quantise(q_codes[:], q_scales[:], q_grouped[:].rearrange("p t m j -> p (t m) j"))
@@ -102,69 +105,42 @@ def tile_attend_adcheads_kernel(tc, query, book, fac, pat, offs, out):
         def cast(n, c0, c1, copy):
             interleave(copy, book_grouped[n][:, c0:c1, :], book_raw[n][:, :, c0:c1])
 
-        def quantise_book(n):
-            cols = slice(starts[n], starts[n] + BOOK_LOADS[n])
-            quantise(book_codes[:, cols], book_scales[:, cols], book_grouped[n][:])
+        def quantise_book(n, c0, c1):
+            cols = slice(starts[n] + c0, starts[n] + c1)
+            quantise(book_codes[:, cols], book_scales[:, cols], book_grouped[n][:, c0:c1, :])
 
-        outer = [psum.tile([P, BANK], F32, name="outer%d" % t, tag="bank%d" % t) for t in range(PACK)]
-        inner = [psum.tile([P, BANK], F32, name="inner%d" % t, tag="bank%d" % (PACK + t)) for t in range(PACK)]
-        places = [(outer, 0), (outer, 128), (inner, 0), (inner, 256), (outer, 384)]
-        places_first = [(outer, 0), (outer, 128), (inner, 0), (outer, 0), (inner, 256)]
+        lower = [psum.tile([P, BANK], F32, name="lower%d" % t, tag="bank%d" % t) for t in range(PACK)]
+        upper = [psum.tile([P, BANK], F32, name="upper%d" % t, tag="bank%d" % (PACK + t)) for t in range(PACK)]
 
-        def score(n, t):
-            banks, c0 = (places if t > 0 else places_first)[n]
-            width = BOOK_LOADS[n]
-            product(banks[t][:, c0 : c0 + width], q_mx, slice(P * t, P * (t + 1)), book_mx, slice(starts[n], starts[n] + width))
+        def score(acc, t, c0, c1):
+            product(acc, q_mx, slice(P * t, P * (t + 1)), book_mx, slice(c0, c1))
 
-        def drain(loads, t, copy):
-            banks, c0 = (places if t > 0 else places_first)[loads[0]]
-            width = sum(BOOK_LOADS[n] for n in loads)
-            copy(scores[t][:, starts[loads[0]] : starts[loads[0]] + width], banks[t][:, c0 : c0 + width])
-
-        cast(0, 0, UNIT, nc.scalar.copy)
-        quantise_book(0)
-        for t in range(PACK):
-            score(0, t)
-        fac_early = keep.tile([P, 2, 2 * PIECE], F32, tag="book_raw0")
-        nc.scalar.copy(fac_early[:], fac_sb[:, 0:2].unsqueeze(2).to_broadcast([P, 2, 2 * PIECE]))
-        fac_wide = (fac_early, fac_late)
-        cast(1, 0, 160, nc.vector.tensor_copy)
-        cast(1, 160, 256, nc.scalar.copy)
-        quantise_book(1)
-        for t in range(PACK):
-            score(1, t)
-        cast(2, 0, 160, nc.vector.tensor_copy)
-        cast(2, 160, 256, nc.scalar.copy)
-        quantise_book(2)
-        for t in range(PACK):
-            score(2, t)
-        cast(3, 0, 2 * UNIT, nc.vector.tensor_copy)
-        cast(4, 0, UNIT, nc.vector.tensor_copy)
-        quantise_book(3)
-        quantise_book(4)
-        drain((0, 1), 0, nc.scalar.copy)
-        drain((2,), 0, nc.scalar.copy)
-        score(3, 0)
-        score(4, 0)
-        drain((3,), 0, nc.scalar.copy)
-        drain((4,), 0, nc.vector.tensor_copy)
-        for t in (1, 2, 3):
-            drain((0, 1), t, nc.scalar.copy)
-        for t in (1, 2, 3):
-            score(3, t)
-            score(4, t)
+        banks = (lower, upper)
+        for n in (0, 1):
+            cast(n, 0, 256, nc.vector.tensor_copy)
+            cast(n, 256, 384, nc.scalar.copy if n == 0 else nc.vector.tensor_copy)
+            quantise_book(n, 0, 256)
+            quantise_book(n, 256, 384)
+            for t in range(PACK):
+                score(banks[n][t][:, 0:256], t, starts[n], starts[n] + 256)
+                score(banks[n][t][:, 256:384], t, starts[n] + 256, starts[n] + 384)
+            for t in range(PACK):
+                nc.scalar.copy(scores[t][:, starts[n] : starts[n] + 384], banks[n][t][:, 0:384])
+        for c0 in (0, 128):
+            cast(2, c0, c0 + 128, nc.vector.tensor_copy)
+        for u in (0, 1):
+            quantise_book(2, 128 * u, 128 * (u + 1))
+            cols = slice(768 + 128 * u, 768 + 128 * (u + 1))
+            score(lower[u][:, 0:128], 0, cols.start, cols.stop)
+            nc.vector.tensor_copy(scores[0][:, cols], lower[u][:, 0:128])
+        for t, bank in ((1, upper[0]), (2, lower[2]), (3, lower[3])):
+            score(bank[:, 0:256], t, 768, C)
+            nc.scalar.copy(scores[t][:, 768:C], bank[:, 0:256])
 
         pat_grouped = keep.tile([P, M, PACK], BF16, align_bytes=64)
         interleave(nc.vector.tensor_copy, pat_grouped[:], pat_raw[:])
         quantise(q_codes[:, 0:M], q_scales[:, 0:M], pat_grouped[:])
         pat_mx = q_mx
-
-        drain((2, 3), 1, nc.scalar.copy)
-        drain((4,), 1, nc.scalar.copy)
-        for t in (2, 3):
-            drain((2, 3), t, nc.scalar.copy)
-        for t in (2, 3):
-            drain((4,), t, nc.scalar.copy)
 
         looked = [keep.tile([P, PACK, 2 * PIECE], F32, name="looked%d" % h, tag="looked%d" % h, align_bytes=64) for h in range(2)]
 
@@ -201,4 +177,4 @@ def tile_attend_adcheads_kernel(tc, query, book, fac, pat, offs, out):
         fourth = keep.tile([P, PIECE, PACK], BF16, tag="looked0", align_bytes=64)
         interleave(nc.vector.tensor_copy, fourth[:], looked[1][:, :, PIECE : 2 * PIECE])
         finish("third", third[:], 2 * PIECE, PIECE, "third_codes", 1, nc.scalar.copy)
-        finish("fourth", fourth[:], 3 * PIECE, PIECE, "looked1", 4, nc.vector.tensor_copy)
+        finish("fourth", fourth[:], 3 * PIECE, PIECE, "looked1", 5, nc.vector.tensor_copy)

@@ -19,7 +19,7 @@ PACK = 4
 QUAD = 32
 UNIT = 128
 BANK = 512
-BOOK_LOADS = (384, 384, 256)
+BOOK_LOADS = (256, 384, 256, 128)
 PIECE = 128
 PIECES = I // PIECE
 
@@ -74,11 +74,9 @@ def tile_attend_adcheads_kernel(tc, query, book, fac, pat, offs, out):
         offsets = keep.tile([P, I // 16], U16)
         nc.sync.dma_start(offsets[:], offs)
 
-        fac_late = keep.tile([P, 2, PIECE], F32)
-        nc.scalar.copy(fac_late[:], fac_sb[:, 2:4].unsqueeze(2).to_broadcast([P, 2, PIECE]))
+        fac_wide = keep.tile([P, PACK, 2 * PIECE], F32)
+        nc.scalar.copy(fac_wide[:, 0, :], fac_sb[:, 0:1].to_broadcast([P, 2 * PIECE]))
 
-        fac_early = keep.tile([P, 2, 2 * PIECE], F32)
-        fac_wide = (fac_early, fac_late)
         q_grouped = keep.tile([P, PACK, P, PACK], BF16, align_bytes=64)
         nc.vector.memset(q_grouped[:], 0.0)
         for quad in (0, 2, 3, 1):
@@ -88,14 +86,14 @@ def tile_attend_adcheads_kernel(tc, query, book, fac, pat, offs, out):
                 q_grouped[parts, :, parts, :].rearrange("p t m j -> p m j t"),
                 q_raw[parts, :, :].rearrange("p j (m t) -> p m j t", t=PACK),
             )
-        nc.scalar.copy(fac_early[:], fac_sb[:, 0:2].unsqueeze(2).to_broadcast([P, 2, 2 * PIECE]))
+        nc.scalar.copy(fac_wide[:, 1:PACK, :], fac_sb[:, 1:PACK].unsqueeze(2).to_broadcast([P, PACK - 1, 2 * PIECE]))
         q_codes = keep.tile([P, Q], U32, align_bytes=64)
         q_scales = keep.tile([P, Q], U8, align_bytes=64)
         quantise(q_codes[:], q_scales[:], q_grouped[:].rearrange("p t m j -> p (t m) j"))
         q_mx = (q_codes, q_scales)
 
         scores = [keep.tile([P, C], F32, name="scores%d" % t) for t in range(PACK)]
-        book_codes = keep.tile([P, C], U32, align_bytes=64)
+        book_codes = keep.tile([P, C], U32, tag="book_codes", align_bytes=64)
         book_scales = keep.tile([P, C], U8, align_bytes=64)
         book_mx = (book_codes, book_scales)
 
@@ -115,46 +113,63 @@ def tile_attend_adcheads_kernel(tc, query, book, fac, pat, offs, out):
         def score(acc, t, c0, c1):
             product(acc, q_mx, slice(P * t, P * (t + 1)), book_mx, slice(c0, c1))
 
-        banks = (lower, upper)
-        for n in (0, 1):
-            cast(n, 0, 256, nc.vector.tensor_copy)
-            cast(n, 256, 384, nc.scalar.copy if n == 0 else nc.vector.tensor_copy)
-            quantise_book(n, 0, 256)
-            quantise_book(n, 256, 384)
-            for t in range(PACK):
-                score(banks[n][t][:, 0:256], t, starts[n], starts[n] + 256)
-                score(banks[n][t][:, 256:384], t, starts[n] + 256, starts[n] + 384)
-            for t in range(PACK):
-                nc.scalar.copy(scores[t][:, starts[n] : starts[n] + 384], banks[n][t][:, 0:384])
-        for c0 in (0, 128):
-            cast(2, c0, c0 + 128, nc.vector.tensor_copy)
-        for u in (0, 1):
-            quantise_book(2, 128 * u, 128 * (u + 1))
-            cols = slice(768 + 128 * u, 768 + 128 * (u + 1))
-            score(lower[u][:, 0:128], 0, cols.start, cols.stop)
-            nc.vector.tensor_copy(scores[0][:, cols], lower[u][:, 0:128])
-        for t, bank in ((1, upper[0]), (2, lower[2]), (3, lower[3])):
-            score(bank[:, 0:256], t, 768, C)
-            nc.scalar.copy(scores[t][:, 768:C], bank[:, 0:256])
-
+        cast(0, 0, 160, nc.vector.tensor_copy)
+        cast(0, 160, 256, nc.scalar.copy)
+        quantise_book(0, 0, 256)
+        for t in range(PACK):
+            score(lower[t][:, 0:256], t, 0, 256)
+        for t in range(PACK):
+            nc.scalar.copy(scores[t][:, 0:256], lower[t][:, 0:256])
+        cast(1, 0, 256, nc.vector.tensor_copy)
+        cast(1, 256, 384, nc.vector.tensor_copy)
+        quantise_book(1, 0, 256)
+        cast(2, 0, 128, nc.vector.tensor_copy)
+        cast(2, 128, 256, nc.scalar.copy)
+        quantise_book(1, 256, 384)
+        for t in range(PACK):
+            score(upper[t][:, 0:256], t, 256, 512)
+            score(upper[t][:, 256:384], t, 512, 640)
+        for t in range(PACK):
+            nc.scalar.copy(scores[t][:, 256:640], upper[t][:, 0:384])
+        cast(3, 0, 128, nc.vector.tensor_copy)
+        quantise_book(2, 0, 256)
+        quantise_book(3, 0, 128)
+        score(lower[0][:, 0:256], 0, 640, 896)
+        score(upper[0][:, 0:128], 0, 896, C)
         pat_grouped = keep.tile([P, M, PACK], BF16, align_bytes=64)
         interleave(nc.vector.tensor_copy, pat_grouped[:], pat_raw[:])
+        nc.vector.tensor_copy(scores[0][:, 640:896], lower[0][:, 0:256])
+        nc.vector.tensor_copy(scores[0][:, 896:C], upper[0][:, 0:128])
+        for t in (1, 2, 3):
+            score(lower[t][:, 256:384], t, 896, C)
+            score(lower[t][:, 0:256], t, 640, 896)
+            nc.scalar.copy(scores[t][:, 640:C], lower[t][:, 0:384])
         quantise(q_codes[:, 0:M], q_scales[:, 0:M], pat_grouped[:])
         pat_mx = q_mx
 
+        fac_second = keep.tile([P, 6 * PIECE], F32, tag="book_codes", align_bytes=64)
+        nc.scalar.copy(
+            fac_second[:, 0 : 4 * PIECE].rearrange("p (t c) -> p t c", t=2),
+            fac_sb[:, 0:2].unsqueeze(2).to_broadcast([P, 2, 2 * PIECE]),
+        )
+        nc.scalar.copy(
+            fac_second[:, 4 * PIECE : 6 * PIECE].rearrange("p (t c) -> p t c", t=2),
+            fac_sb[:, 2:4].unsqueeze(2).to_broadcast([P, 2, PIECE]),
+        )
+        second_starts = (0, 2 * PIECE, 4 * PIECE, 5 * PIECE)
         looked = [keep.tile([P, PACK, 2 * PIECE], F32, name="looked%d" % h, tag="looked%d" % h, align_bytes=64) for h in range(2)]
 
         def look_up(s0, width, t):
             piece = offsets[:, s0 // 16 : (s0 + width) // 16]
             c0 = s0 % (2 * PIECE)
-            nc.vector.tensor_tensor(
-                looked[s0 // (2 * PIECE)][:, t, c0 : c0 + width], scores[t][:].indirect(piece), fac_wide[t // 2][:, t % 2, :], MULT
-            )
+            factors = fac_wide[:, t, :] if s0 == 0 else fac_second[:, second_starts[t] : second_starts[t] + width]
+            nc.vector.tensor_tensor(looked[s0 // (2 * PIECE)][:, t, c0 : c0 + width], scores[t][:].indirect(piece), factors, MULT)
 
+        for t in range(PACK):
+            look_up(0, 2 * PIECE, t)
         for t in (0, 1):
-            for h in range(2):
-                look_up(2 * PIECE * h, 2 * PIECE, t)
-        for k in range(PIECES):
+            look_up(2 * PIECE, 2 * PIECE, t)
+        for k in (2, 3):
             for t in (2, 3):
                 look_up(PIECE * k, PIECE, t)
 
@@ -169,8 +184,7 @@ def tile_attend_adcheads_kernel(tc, query, book, fac, pat, offs, out):
             nc.sync.dma_start(out[:, s0 : s0 + width], result[:])
 
         first = keep.tile([P, 2 * PIECE, PACK], BF16, align_bytes=64)
-        for k in (0, 1):
-            interleave(nc.scalar.copy, first[:, k * PIECE : (k + 1) * PIECE, :], looked[0][:, :, k * PIECE : (k + 1) * PIECE])
+        interleave(nc.scalar.copy, first[:], looked[0][:])
         third = keep.tile([P, PIECE, PACK], BF16, align_bytes=64)
         interleave(nc.scalar.copy, third[:], looked[1][:, :, 0:PIECE])
         finish("first", first[:], 0, 2 * PIECE, "first_codes", 0, nc.scalar.copy)

@@ -108,7 +108,7 @@ def tile_attend_adcheads_kernel(tc, query, book, fac, pat, offs, out):
             quantise(book_codes[:, cols], book_scales[:, cols], book_grouped[n][:, c0:c1, :])
 
         lower = [psum.tile([P, BANK], F32, name="lower%d" % t, tag="bank%d" % t) for t in range(PACK)]
-        upper = [psum.tile([P, BANK], F32, name="upper%d" % t, tag="bank%d" % (PACK + t)) for t in range(PACK)]
+        upper = [psum.tile([P, BANK], F32, name="upper%d" % t, tag="bank%d" % (PACK + t)) for t in range(PACK - 1)]
 
         def score(acc, t, c0, c1):
             product(acc, q_mx, slice(P * t, P * (t + 1)), book_mx, slice(c0, c1))
@@ -123,13 +123,13 @@ def tile_attend_adcheads_kernel(tc, query, book, fac, pat, offs, out):
         cast(1, 0, 256, nc.vector.tensor_copy)
         cast(1, 256, 384, nc.vector.tensor_copy)
         quantise_book(1, 0, 256)
+        quantise_book(1, 256, 384)
         cast(2, 0, 128, nc.vector.tensor_copy)
         cast(2, 128, 256, nc.scalar.copy)
-        quantise_book(1, 256, 384)
-        for t in range(PACK):
+        for t in range(PACK - 1):
             score(upper[t][:, 0:256], t, 256, 512)
             score(upper[t][:, 256:384], t, 512, 640)
-        for t in range(PACK):
+        for t in range(PACK - 1):
             nc.scalar.copy(scores[t][:, 256:640], upper[t][:, 0:384])
         cast(3, 0, 128, nc.vector.tensor_copy)
         quantise_book(2, 0, 256)
@@ -143,6 +143,10 @@ def tile_attend_adcheads_kernel(tc, query, book, fac, pat, offs, out):
         for t in (1, 2, 3):
             score(lower[t][:, 256:384], t, 896, C)
             score(lower[t][:, 0:256], t, 640, 896)
+            if t == 3:
+                score(lower[0][:, 0:256], t, 256, 512)
+                score(lower[0][:, 256:384], t, 512, 640)
+                nc.scalar.copy(scores[t][:, 256:640], lower[0][:, 0:384])
             nc.scalar.copy(scores[t][:, 640:C], lower[t][:, 0:384])
         quantise(q_codes[:, 0:M], q_scales[:, 0:M], pat_grouped[:])
         pat_mx = q_mx
@@ -187,7 +191,7 @@ def tile_attend_adcheads_kernel(tc, query, book, fac, pat, offs, out):
         interleave(nc.scalar.copy, first[:], looked[0][:])
         third = keep.tile([P, PIECE, PACK], BF16, align_bytes=64)
         interleave(nc.scalar.copy, third[:], looked[1][:, :, 0:PIECE])
-        finish("first", first[:], 0, 2 * PIECE, "first_codes", 0, nc.scalar.copy)
+        finish("first", first[:], 0, 2 * PIECE, "first_codes", 7, nc.scalar.copy)
         fourth = keep.tile([P, PIECE, PACK], BF16, tag="looked0", align_bytes=64)
         interleave(nc.vector.tensor_copy, fourth[:], looked[1][:, :, PIECE : 2 * PIECE])
         finish("third", third[:], 2 * PIECE, PIECE, "third_codes", 1, nc.scalar.copy)

@@ -17,11 +17,9 @@ MULT = mybir.AluOpType.mult
 P = 128
 PACK = 4
 QUAD = 32
-UNIT = 128
 BANK = 512
-BOOK_LOADS = (256, 384, 256, 128)
 PIECE = 128
-PIECES = I // PIECE
+BOOK_LOADS = (256, 384, 256, 128)
 
 
 def interleave(engine_copy, grouped, planes):
@@ -62,20 +60,24 @@ def tile_attend_adcheads_kernel(tc, query, book, fac, pat, offs, out):
                 query[rows, rows].rearrange("(p j) c -> p j c", j=PACK),
             )
         book_rows = book.rearrange("(p j) c -> p j c", j=PACK)
+        starts = [sum(BOOK_LOADS[:n]) for n in range(len(BOOK_LOADS))]
         book_raw = []
-        c0 = 0
         for n, width in enumerate(BOOK_LOADS):
-            raw = keep.tile([P, PACK, width], F32, name="book_raw%d" % n, tag="book_raw%d" % n)
-            nc.sync.dma_start(raw[:], book_rows[:, :, c0 : c0 + width])
+            raw = keep.tile([P, PACK, width], F32, name="book_raw%d" % n, tag="book_raw%d" % n, align_bytes=64)
+            nc.sync.dma_start(raw[:], book_rows[:, :, starts[n] : starts[n] + width])
             book_raw.append(raw)
-            c0 = c0 + width
         pat_raw = keep.tile([P, PACK, M], F32)
         nc.sync.dma_start(pat_raw[:], pat.rearrange("(p j) m -> p j m", j=PACK))
         offsets = keep.tile([P, I // 16], U16)
         nc.sync.dma_start(offsets[:], offs)
 
-        fac_wide = keep.tile([P, PACK, 2 * PIECE], F32)
-        nc.scalar.copy(fac_wide[:, 0, :], fac_sb[:, 0:1].to_broadcast([P, 2 * PIECE]))
+        def spread(wide, t0, t1):
+            nc.scalar.copy(wide, fac_sb[:, t0:t1].unsqueeze(2).to_broadcast([P, t1 - t0, wide.shape[2]]))
+
+        looked = [keep.tile([P, PACK, 2 * PIECE], F32, name="looked%d" % h, tag="looked%d" % h, align_bytes=64) for h in range(2)]
+        fac_low = keep.tile([P, 3, 2 * PIECE], F32)
+        fac_high = keep.tile([P, 1, PIECE], F32)
+        spread(fac_low[:, 0:1, :], 0, 1)
 
         q_grouped = keep.tile([P, PACK, P, PACK], BF16, align_bytes=64)
         nc.vector.memset(q_grouped[:], 0.0)
@@ -86,19 +88,18 @@ def tile_attend_adcheads_kernel(tc, query, book, fac, pat, offs, out):
                 q_grouped[parts, :, parts, :].rearrange("p t m j -> p m j t"),
                 q_raw[parts, :, :].rearrange("p j (m t) -> p m j t", t=PACK),
             )
-        nc.scalar.copy(fac_wide[:, 1:PACK, :], fac_sb[:, 1:PACK].unsqueeze(2).to_broadcast([P, PACK - 1, 2 * PIECE]))
+        spread(fac_low[:, 1:3, :], 1, 3)
+        spread(fac_high[:], 3, 4)
+        spread(looked[1][:, 2:3, :], 3, 4)
         q_codes = keep.tile([P, Q], U32, align_bytes=64)
         q_scales = keep.tile([P, Q], U8, align_bytes=64)
         quantise(q_codes[:], q_scales[:], q_grouped[:].rearrange("p t m j -> p (t m) j"))
         q_mx = (q_codes, q_scales)
 
-        scores = [keep.tile([P, C], F32, name="scores%d" % t) for t in range(PACK)]
-        book_codes = keep.tile([P, C], U32, tag="book_codes", align_bytes=64)
+        book_codes = keep.tile([P, C], U32, align_bytes=64)
         book_scales = keep.tile([P, C], U8, align_bytes=64)
         book_mx = (book_codes, book_scales)
-
-        starts = [sum(BOOK_LOADS[:n]) for n in range(len(BOOK_LOADS))]
-        book_grouped = [keep.tile([P, width, PACK], BF16, name="book_grouped%d" % n, align_bytes=64) for n, width in enumerate(BOOK_LOADS)]
+        book_grouped = [keep.tile([P, width, PACK], BF16, name="book_grouped%d" % n, tag="book_grouped%d" % n, align_bytes=64) for n, width in enumerate(BOOK_LOADS)]
 
         def cast(n, c0, c1, copy):
             interleave(copy, book_grouped[n][:, c0:c1, :], book_raw[n][:, :, c0:c1])
@@ -107,75 +108,79 @@ def tile_attend_adcheads_kernel(tc, query, book, fac, pat, offs, out):
             cols = slice(starts[n] + c0, starts[n] + c1)
             quantise(book_codes[:, cols], book_scales[:, cols], book_grouped[n][:, c0:c1, :])
 
-        lower = [psum.tile([P, BANK], F32, name="lower%d" % t, tag="bank%d" % t) for t in range(PACK)]
-        upper = [psum.tile([P, BANK], F32, name="upper%d" % t, tag="bank%d" % (PACK + t)) for t in range(PACK - 1)]
+        def bank(name, number):
+            return psum.tile([P, BANK], F32, name=name, tag="bank%d" % number)
 
         def score(acc, t, c0, c1):
             product(acc, q_mx, slice(P * t, P * (t + 1)), book_mx, slice(c0, c1))
 
+        early, middle, last = bank("early", 0), bank("middle", 4), bank("last", 7)
+        lower = {t: bank("lower%d" % t, t) for t in (1, 2)}
+        upper = {t: bank("upper%d" % t, PACK + t) for t in (1, 2)}
+
         cast(0, 0, 160, nc.vector.tensor_copy)
         cast(0, 160, 256, nc.scalar.copy)
         quantise_book(0, 0, 256)
-        for t in range(PACK):
+        score(early[:, 0:256], 0, 0, 256)
+        for t in (1, 2):
             score(lower[t][:, 0:256], t, 0, 256)
-        for t in range(PACK):
-            nc.scalar.copy(scores[t][:, 0:256], lower[t][:, 0:256])
         cast(1, 0, 256, nc.vector.tensor_copy)
-        cast(1, 256, 384, nc.vector.tensor_copy)
-        quantise_book(1, 0, 256)
+        cast(1, 256, 384, nc.scalar.copy)
         quantise_book(1, 256, 384)
+        quantise_book(1, 0, 256)
+        scores = {
+            0: keep.tile([P, C], F32, name="scores0", tag="book_raw1", align_bytes=64),
+            1: keep.tile([P, C], F32, name="scores1"),
+            3: keep.tile([P, C], F32, name="scores3"),
+        }
+        nc.scalar.copy(scores[0][:, 0:256], early[:, 0:256])
+        score(middle[:, 256:384], 0, 512, 640)
+        score(middle[:, 0:256], 0, 256, 512)
+        for t in (1, 2):
+            score(lower[t][:, 256:512], t, 256, 512)
         cast(2, 0, 128, nc.vector.tensor_copy)
         cast(2, 128, 256, nc.scalar.copy)
-        for t in range(PACK - 1):
-            score(upper[t][:, 0:256], t, 256, 512)
-            score(upper[t][:, 256:384], t, 512, 640)
-        for t in range(PACK - 1):
-            nc.scalar.copy(scores[t][:, 256:640], upper[t][:, 0:384])
+        nc.scalar.copy(scores[0][:, 256:640], middle[:, 0:384])
+        nc.scalar.copy(scores[1][:, 0:BANK], lower[1][:])
         cast(3, 0, 128, nc.vector.tensor_copy)
         quantise_book(2, 0, 256)
         quantise_book(3, 0, 128)
-        score(lower[0][:, 0:256], 0, 640, 896)
-        score(upper[0][:, 0:128], 0, 896, C)
-        pat_grouped = keep.tile([P, M, PACK], BF16, align_bytes=64)
+        score(early[:, 0:256], 0, 640, 896)
+        score(last[:, 0:128], 0, 896, C)
+        pat_grouped = keep.tile([P, M, PACK], BF16, tag="book_grouped3", align_bytes=64)
         interleave(nc.vector.tensor_copy, pat_grouped[:], pat_raw[:])
-        nc.vector.tensor_copy(scores[0][:, 640:896], lower[0][:, 0:256])
-        nc.vector.tensor_copy(scores[0][:, 896:C], upper[0][:, 0:128])
+        nc.scalar.copy(scores[0][:, 640:896], early[:, 0:256])
+        nc.vector.tensor_copy(scores[0][:, 896:C], last[:, 0:128])
+        pat_codes = keep.tile([P, M], U32, align_bytes=64)
+        pat_scales = keep.tile([P, M], U8, align_bytes=64)
+        quantise(pat_codes[:], pat_scales[:], pat_grouped[:])
+        pat_mx = (pat_codes, pat_scales)
+        scores[2] = keep.tile([P, C], F32, name="scores2", tag="book_grouped3", align_bytes=64)
+        lower[3] = bank("lower3", 0)
+        upper[3] = bank("upper3", 3)
         for t in (1, 2, 3):
-            score(lower[t][:, 256:384], t, 896, C)
-            score(lower[t][:, 0:256], t, 640, 896)
-            if t == 3:
-                score(lower[0][:, 0:256], t, 256, 512)
-                score(lower[0][:, 256:384], t, 512, 640)
-                nc.scalar.copy(scores[t][:, 256:640], lower[0][:, 0:384])
-            nc.scalar.copy(scores[t][:, 640:C], lower[t][:, 0:384])
-        quantise(q_codes[:, 0:M], q_scales[:, 0:M], pat_grouped[:])
-        pat_mx = q_mx
+            score(upper[t][:], t, BANK, C)
+        score(lower[3][:], 3, 0, BANK)
+        nc.scalar.copy(scores[1][:, BANK:C], upper[1][:])
+        nc.scalar.copy(scores[2][:, 0:BANK], lower[2][:])
+        nc.scalar.copy(scores[2][:, BANK:C], upper[2][:])
+        nc.scalar.copy(scores[3][:, BANK:C], upper[3][:])
+        nc.scalar.copy(scores[3][:, 0:BANK], lower[3][:])
 
-        fac_second = keep.tile([P, 6 * PIECE], F32, tag="book_codes", align_bytes=64)
-        nc.scalar.copy(
-            fac_second[:, 0 : 4 * PIECE].rearrange("p (t c) -> p t c", t=2),
-            fac_sb[:, 0:2].unsqueeze(2).to_broadcast([P, 2, 2 * PIECE]),
-        )
-        nc.scalar.copy(
-            fac_second[:, 4 * PIECE : 6 * PIECE].rearrange("p (t c) -> p t c", t=2),
-            fac_sb[:, 2:4].unsqueeze(2).to_broadcast([P, 2, PIECE]),
-        )
-        second_starts = (0, 2 * PIECE, 4 * PIECE, 5 * PIECE)
-        looked = [keep.tile([P, PACK, 2 * PIECE], F32, name="looked%d" % h, tag="looked%d" % h, align_bytes=64) for h in range(2)]
-
-        def look_up(s0, width, t):
+        def look_up(s0, width, t, factors):
             piece = offsets[:, s0 // 16 : (s0 + width) // 16]
             c0 = s0 % (2 * PIECE)
-            factors = fac_wide[:, t, :] if s0 == 0 else fac_second[:, second_starts[t] : second_starts[t] + width]
             nc.vector.tensor_tensor(looked[s0 // (2 * PIECE)][:, t, c0 : c0 + width], scores[t][:].indirect(piece), factors, MULT)
 
-        for t in range(PACK):
-            look_up(0, 2 * PIECE, t)
         for t in (0, 1):
-            look_up(2 * PIECE, 2 * PIECE, t)
+            for h in (0, 1):
+                look_up(2 * PIECE * h, 2 * PIECE, t, fac_low[:, t, :])
+        look_up(0, 2 * PIECE, 2, fac_low[:, 2, :])
+        for k in (0, 1):
+            look_up(PIECE * k, PIECE, 3, looked[1][:, 2, PIECE * k : PIECE * (k + 1)])
         for k in (2, 3):
-            for t in (2, 3):
-                look_up(PIECE * k, PIECE, t)
+            look_up(PIECE * k, PIECE, 2, fac_low[:, 2, 0:PIECE])
+            look_up(PIECE * k, PIECE, 3, fac_high[:, 0, :])
 
         def finish(name, grouped, s0, width, codes_tag, bank, copy):
             codes = keep.tile([P, width], U32, name=name + "_codes", tag=codes_tag, align_bytes=64)
@@ -188,11 +193,12 @@ def tile_attend_adcheads_kernel(tc, query, book, fac, pat, offs, out):
             nc.sync.dma_start(out[:, s0 : s0 + width], result[:])
 
         first = keep.tile([P, 2 * PIECE, PACK], BF16, align_bytes=64)
-        interleave(nc.scalar.copy, first[:], looked[0][:])
+        interleave(nc.scalar.copy, first[:, 0:PIECE, :], looked[0][:, :, 0:PIECE])
+        interleave(nc.scalar.copy, first[:, PIECE : 2 * PIECE, :], looked[0][:, :, PIECE : 2 * PIECE])
         third = keep.tile([P, PIECE, PACK], BF16, align_bytes=64)
         interleave(nc.scalar.copy, third[:], looked[1][:, :, 0:PIECE])
         finish("first", first[:], 0, 2 * PIECE, "first_codes", 7, nc.scalar.copy)
         fourth = keep.tile([P, PIECE, PACK], BF16, tag="looked0", align_bytes=64)
         interleave(nc.vector.tensor_copy, fourth[:], looked[1][:, :, PIECE : 2 * PIECE])
         finish("third", third[:], 2 * PIECE, PIECE, "third_codes", 1, nc.scalar.copy)
-        finish("fourth", fourth[:], 3 * PIECE, PIECE, "looked1", 5, nc.vector.tensor_copy)
+        finish("fourth", fourth[:], 3 * PIECE, PIECE, "looked1", 4, nc.vector.tensor_copy)

@@ -50,10 +50,10 @@ def tile_attend_adcheads_kernel(tc, query, book, fac, pat, offs, out):
             )
 
         fac_sb = keep.tile([P, PACK], F32)
-        nc.scalar.dma_start(fac_sb[:], fac.rearrange("(p t) o -> p (t o)", t=PACK))
+        nc.sync.dma_start(fac_sb[:], fac.rearrange("(p t) o -> p (t o)", t=PACK))
         q_raw = keep.tile([P, PACK, P], F32)
-        for quad in (0, 2, 3, 1):
-            queue = nc.scalar if quad == 2 else nc.sync
+        for quad in (0, 2, 1, 3):
+            queue = nc.scalar if quad >= 2 else nc.sync
             rows = slice(P * quad, P * (quad + 1))
             queue.dma_start(
                 q_raw[QUAD * quad : QUAD * (quad + 1), :, :],
@@ -66,7 +66,7 @@ def tile_attend_adcheads_kernel(tc, query, book, fac, pat, offs, out):
             raw = keep.tile([P, PACK, width], F32, name="book_raw%d" % n, tag="book_raw%d" % n, align_bytes=64)
             nc.sync.dma_start(raw[:], book_rows[:, :, starts[n] : starts[n] + width])
             book_raw.append(raw)
-        pat_raw = keep.tile([P, PACK, M], F32)
+        pat_raw = keep.tile([P, PACK, M], F32, tag="pat_raw")
         nc.sync.dma_start(pat_raw[:], pat.rearrange("(p j) m -> p j m", j=PACK))
         offsets = keep.tile([P, I // 16], U16)
         nc.sync.dma_start(offsets[:], offs)
@@ -115,14 +115,14 @@ def tile_attend_adcheads_kernel(tc, query, book, fac, pat, offs, out):
             product(acc, q_mx, slice(P * t, P * (t + 1)), book_mx, slice(c0, c1))
 
         early, middle, last = bank("early", 0), bank("middle", 4), bank("last", 7)
-        lower = {t: bank("lower%d" % t, t) for t in (1, 2)}
+        lower = {t: bank("lower%d" % t, t) for t in (1, 2, 3)}
         upper = {t: bank("upper%d" % t, PACK + t) for t in (1, 2)}
 
         cast(0, 0, 160, nc.vector.tensor_copy)
         cast(0, 160, 256, nc.scalar.copy)
         quantise_book(0, 0, 256)
         score(early[:, 0:256], 0, 0, 256)
-        for t in (1, 2):
+        for t in (1, 2, 3):
             score(lower[t][:, 0:256], t, 0, 256)
         cast(1, 0, 256, nc.vector.tensor_copy)
         cast(1, 256, 384, nc.scalar.copy)
@@ -131,12 +131,11 @@ def tile_attend_adcheads_kernel(tc, query, book, fac, pat, offs, out):
         scores = {
             0: keep.tile([P, C], F32, name="scores0", tag="book_raw1", align_bytes=64),
             1: keep.tile([P, C], F32, name="scores1"),
-            3: keep.tile([P, C], F32, name="scores3"),
         }
         nc.scalar.copy(scores[0][:, 0:256], early[:, 0:256])
         score(middle[:, 256:384], 0, 512, 640)
         score(middle[:, 0:256], 0, 256, 512)
-        for t in (1, 2):
+        for t in (1, 2, 3):
             score(lower[t][:, 256:512], t, 256, 512)
         cast(2, 0, 128, nc.vector.tensor_copy)
         cast(2, 128, 256, nc.scalar.copy)
@@ -156,16 +155,15 @@ def tile_attend_adcheads_kernel(tc, query, book, fac, pat, offs, out):
         quantise(pat_codes[:], pat_scales[:], pat_grouped[:])
         pat_mx = (pat_codes, pat_scales)
         scores[2] = keep.tile([P, C], F32, name="scores2", tag="book_grouped3", align_bytes=64)
-        lower[3] = bank("lower3", 0)
-        upper[3] = bank("upper3", 3)
+        scores[3] = keep.tile([P, C], F32, name="scores3", tag="pat_raw")
+        upper[3] = bank("upper3", 4)
         for t in (1, 2, 3):
             score(upper[t][:], t, BANK, C)
-        score(lower[3][:], 3, 0, BANK)
         nc.scalar.copy(scores[1][:, BANK:C], upper[1][:])
         nc.scalar.copy(scores[2][:, 0:BANK], lower[2][:])
         nc.scalar.copy(scores[2][:, BANK:C], upper[2][:])
-        nc.scalar.copy(scores[3][:, BANK:C], upper[3][:])
         nc.scalar.copy(scores[3][:, 0:BANK], lower[3][:])
+        nc.scalar.copy(scores[3][:, BANK:C], upper[3][:])
 
         def look_up(s0, width, t, factors):
             piece = offsets[:, s0 // 16 : (s0 + width) // 16]
@@ -201,4 +199,4 @@ def tile_attend_adcheads_kernel(tc, query, book, fac, pat, offs, out):
         fourth = keep.tile([P, PIECE, PACK], BF16, tag="looked0", align_bytes=64)
         interleave(nc.vector.tensor_copy, fourth[:], looked[1][:, :, PIECE : 2 * PIECE])
         finish("third", third[:], 2 * PIECE, PIECE, "third_codes", 1, nc.scalar.copy)
-        finish("fourth", fourth[:], 3 * PIECE, PIECE, "looked1", 4, nc.vector.tensor_copy)
+        finish("fourth", fourth[:], 3 * PIECE, PIECE, "looked1", 0, nc.vector.tensor_copy)

@@ -116,7 +116,8 @@ def tile_attend_adcheads_kernel(tc, query, book, fac, pat, offs, out):
 
         early, middle, last = bank("early", 0), bank("middle", 4), bank("last", 7)
         lower = {t: bank("lower%d" % t, t) for t in (1, 2, 3)}
-        upper = {t: bank("upper%d" % t, PACK + t) for t in (1, 2)}
+        upper = {1: bank("upper1", 5)}
+        third_part = bank("third_part", 6)
 
         cast(0, 0, 160, nc.vector.tensor_copy)
         cast(0, 160, 256, nc.scalar.copy)
@@ -144,18 +145,21 @@ def tile_attend_adcheads_kernel(tc, query, book, fac, pat, offs, out):
         cast(3, 0, 128, nc.vector.tensor_copy)
         quantise_book(2, 0, 256)
         quantise_book(3, 0, 128)
-        score(early[:, 0:256], 0, 640, 896)
+        score(early[:, 0:128], 0, 640, 768)
+        score(third_part[:, 0:128], 0, 768, 896)
         score(last[:, 0:128], 0, 896, C)
         pat_grouped = keep.tile([P, M, PACK], BF16, tag="book_grouped3", align_bytes=64)
         interleave(nc.vector.tensor_copy, pat_grouped[:], pat_raw[:])
-        nc.scalar.copy(scores[0][:, 640:896], early[:, 0:256])
-        nc.vector.tensor_copy(scores[0][:, 896:C], last[:, 0:128])
+        nc.scalar.copy(scores[0][:, 640:768], early[:, 0:128])
+        nc.vector.tensor_copy(scores[0][:, 768:896], third_part[:, 0:128])
+        nc.scalar.copy(scores[0][:, 896:C], last[:, 0:128])
         pat_codes = keep.tile([P, M], U32, align_bytes=64)
         pat_scales = keep.tile([P, M], U8, align_bytes=64)
         quantise(pat_codes[:], pat_scales[:], pat_grouped[:])
         pat_mx = (pat_codes, pat_scales)
         scores[2] = keep.tile([P, C], F32, name="scores2", tag="book_grouped3", align_bytes=64)
         scores[3] = keep.tile([P, C], F32, name="scores3", tag="pat_raw")
+        upper[2] = bank("upper2", 6)
         upper[3] = bank("upper3", 4)
         for t in (1, 2, 3):
             score(upper[t][:], t, BANK, C)

@@ -13,6 +13,7 @@ U16 = mybir.dt.uint16
 U8 = mybir.dt.uint8
 FP8X4 = mybir.dt.float8_e4m3fn_x4
 MULT = mybir.AluOpType.mult
+COPY = mybir.ActivationFunctionType.Copy
 
 P = 128
 PACK = 4
@@ -33,6 +34,7 @@ def tile_attend_adcheads_kernel(tc, query, book, fac, pat, offs, out):
     nc = tc.nc
     with ExitStack() as ctx:
         keep = ctx.enter_context(tc.tile_pool(name="keep", bufs=1))
+        shared = ctx.enter_context(tc.tile_pool(name="shared", bufs=1))
         psum = ctx.enter_context(tc.psum_pool(name="psum", bufs=1))
 
         def quantise(codes, scales, grouped):
@@ -90,7 +92,6 @@ def tile_attend_adcheads_kernel(tc, query, book, fac, pat, offs, out):
             )
         spread(fac_low[:, 1:3, :], 1, 3)
         spread(fac_high[:], 3, 4)
-        spread(looked[1][:, 2:3, :], 3, 4)
         q_codes = keep.tile([P, Q], U32, align_bytes=64)
         q_scales = keep.tile([P, Q], U8, align_bytes=64)
         quantise(q_codes[:], q_scales[:], q_grouped[:].rearrange("p t m j -> p (t m) j"))
@@ -174,18 +175,17 @@ def tile_attend_adcheads_kernel(tc, query, book, fac, pat, offs, out):
             c0 = s0 % (2 * PIECE)
             nc.vector.tensor_tensor(looked[s0 // (2 * PIECE)][:, t, c0 : c0 + width], scores[t][:].indirect(piece), factors, MULT)
 
-        for t in (0, 1):
+        plain = shared.tile([P, 2 * PIECE], F32, offset=512, align_bytes=64)
+        nc.scalar.activation(plain[:], scores[3][:].indirect(offsets[:, 0 : 2 * PIECE // 16]), COPY)
+        nc.scalar.activation(looked[0][:, 3, :], plain[:], COPY, scale=fac_sb[:, 3:4])
+        for t in (0, 1, 2):
             for h in (0, 1):
                 look_up(2 * PIECE * h, 2 * PIECE, t, fac_low[:, t, :])
-        look_up(0, 2 * PIECE, 2, fac_low[:, 2, :])
-        for k in (0, 1):
-            look_up(PIECE * k, PIECE, 3, looked[1][:, 2, PIECE * k : PIECE * (k + 1)])
         for k in (2, 3):
-            look_up(PIECE * k, PIECE, 2, fac_low[:, 2, 0:PIECE])
             look_up(PIECE * k, PIECE, 3, fac_high[:, 0, :])
 
-        def finish(name, grouped, s0, width, codes_tag, bank, copy):
-            codes = keep.tile([P, width], U32, name=name + "_codes", tag=codes_tag, align_bytes=64)
+        def finish(name, grouped, s0, width, bank, copy):
+            codes = keep.tile([P, width], U32, name=name + "_codes", align_bytes=64)
             scales = keep.tile([P, width], U8, name=name + "_scales", align_bytes=64)
             quantise(codes[:], scales[:], grouped)
             acc = psum.tile([P, width], F32, name=name + "_acc", tag="bank%d" % bank)
@@ -195,12 +195,12 @@ def tile_attend_adcheads_kernel(tc, query, book, fac, pat, offs, out):
             nc.sync.dma_start(out[:, s0 : s0 + width], result[:])
 
         first = keep.tile([P, 2 * PIECE, PACK], BF16, align_bytes=64)
+        third = shared.tile([P, PIECE, PACK], BF16, offset=0, align_bytes=64)
+        fourth = shared.tile([P, PIECE, PACK], BF16, offset=1024, align_bytes=64)
         interleave(nc.scalar.copy, first[:, 0:PIECE, :], looked[0][:, :, 0:PIECE])
-        interleave(nc.scalar.copy, first[:, PIECE : 2 * PIECE, :], looked[0][:, :, PIECE : 2 * PIECE])
-        third = keep.tile([P, PIECE, PACK], BF16, align_bytes=64)
         interleave(nc.scalar.copy, third[:], looked[1][:, :, 0:PIECE])
-        finish("first", first[:], 0, 2 * PIECE, "first_codes", 7, nc.scalar.copy)
-        fourth = keep.tile([P, PIECE, PACK], BF16, tag="looked0", align_bytes=64)
+        interleave(nc.vector.tensor_copy, first[:, PIECE : 2 * PIECE, :], looked[0][:, :, PIECE : 2 * PIECE])
         interleave(nc.vector.tensor_copy, fourth[:], looked[1][:, :, PIECE : 2 * PIECE])
-        finish("third", third[:], 2 * PIECE, PIECE, "third_codes", 1, nc.scalar.copy)
-        finish("fourth", fourth[:], 3 * PIECE, PIECE, "looked1", 0, nc.vector.tensor_copy)
+        finish("first", first[:], 0, 2 * PIECE, 7, nc.scalar.copy)
+        finish("fourth", fourth[:], 3 * PIECE, PIECE, 0, nc.scalar.copy)
+        finish("third", third[:], 2 * PIECE, PIECE, 1, nc.vector.tensor_copy)

@@ -20,7 +20,8 @@ PACK = 4
 QUAD = 32
 BANK = 512
 PIECE = 128
-BOOK_LOADS = (256, 384, 256, 128)
+LOAD = 256
+BOOK_LOADS = (LOAD,) * 4
 
 
 def interleave(engine_copy, grouped, planes):
@@ -34,7 +35,6 @@ def tile_attend_adcheads_kernel(tc, query, book, fac, pat, offs, out):
     nc = tc.nc
     with ExitStack() as ctx:
         keep = ctx.enter_context(tc.tile_pool(name="keep", bufs=1))
-        shared = ctx.enter_context(tc.tile_pool(name="shared", bufs=1))
         psum = ctx.enter_context(tc.psum_pool(name="psum", bufs=1))
 
         def quantise(codes, scales, grouped):
@@ -78,7 +78,6 @@ def tile_attend_adcheads_kernel(tc, query, book, fac, pat, offs, out):
 
         looked = [keep.tile([P, PACK, 2 * PIECE], F32, name="looked%d" % h, tag="looked%d" % h, align_bytes=64) for h in range(2)]
         fac_low = keep.tile([P, 3, 2 * PIECE], F32)
-        fac_high = keep.tile([P, 1, PIECE], F32)
         spread(fac_low[:, 0:1, :], 0, 1)
 
         q_grouped = keep.tile([P, PACK, P, PACK], BF16, align_bytes=64)
@@ -91,7 +90,6 @@ def tile_attend_adcheads_kernel(tc, query, book, fac, pat, offs, out):
                 q_raw[parts, :, :].rearrange("p j (m t) -> p m j t", t=PACK),
             )
         spread(fac_low[:, 1:3, :], 1, 3)
-        spread(fac_high[:], 3, 4)
         q_codes = keep.tile([P, Q], U32, align_bytes=64)
         q_scales = keep.tile([P, Q], U8, align_bytes=64)
         quantise(q_codes[:], q_scales[:], q_grouped[:].rearrange("p t m j -> p (t m) j"))
@@ -100,89 +98,91 @@ def tile_attend_adcheads_kernel(tc, query, book, fac, pat, offs, out):
         book_codes = keep.tile([P, C], U32, align_bytes=64)
         book_scales = keep.tile([P, C], U8, align_bytes=64)
         book_mx = (book_codes, book_scales)
-        book_grouped = [keep.tile([P, width, PACK], BF16, name="book_grouped%d" % n, tag="book_grouped%d" % n, align_bytes=64) for n, width in enumerate(BOOK_LOADS)]
+        book_grouped = keep.tile([P, C, PACK], BF16, tag="book_grouped", align_bytes=64)
 
-        def cast(n, c0, c1, copy):
-            interleave(copy, book_grouped[n][:, c0:c1, :], book_raw[n][:, :, c0:c1])
+        def cast(c0, c1, copy):
+            n, at = divmod(c0, LOAD)
+            interleave(copy, book_grouped[:, c0:c1, :], book_raw[n][:, :, at : at + c1 - c0])
 
-        def quantise_book(n, c0, c1):
-            cols = slice(starts[n] + c0, starts[n] + c1)
-            quantise(book_codes[:, cols], book_scales[:, cols], book_grouped[n][:, c0:c1, :])
+        def quantise_book(c0, c1):
+            quantise(book_codes[:, c0:c1], book_scales[:, c0:c1], book_grouped[:, c0:c1, :])
 
-        def bank(name, number):
-            return psum.tile([P, BANK], F32, name=name, tag="bank%d" % number)
-
-        def score(acc, t, c0, c1):
+        def score(t, c0, c1, acc):
             product(acc, q_mx, slice(P * t, P * (t + 1)), book_mx, slice(c0, c1))
 
-        early, middle, last = bank("early", 0), bank("middle", 4), bank("last", 7)
-        lower = {t: bank("lower%d" % t, t) for t in (1, 2, 3)}
-        upper = {1: bank("upper1", 5)}
-        third_part = bank("third_part", 6)
+        def bank(name, number, width):
+            return psum.tile([P, width], F32, name=name, tag="bank%d" % number)
 
-        cast(0, 0, 160, nc.vector.tensor_copy)
-        cast(0, 160, 256, nc.scalar.copy)
-        quantise_book(0, 0, 256)
-        score(early[:, 0:256], 0, 0, 256)
-        for t in (1, 2, 3):
-            score(lower[t][:, 0:256], t, 0, 256)
-        cast(1, 0, 256, nc.vector.tensor_copy)
-        cast(1, 256, 384, nc.scalar.copy)
-        quantise_book(1, 256, 384)
-        quantise_book(1, 0, 256)
-        scores = {
-            0: keep.tile([P, C], F32, name="scores0", tag="book_raw1", align_bytes=64),
-            1: keep.tile([P, C], F32, name="scores1"),
-        }
-        nc.scalar.copy(scores[0][:, 0:256], early[:, 0:256])
-        score(middle[:, 256:384], 0, 512, 640)
-        score(middle[:, 0:256], 0, 256, 512)
-        for t in (1, 2, 3):
-            score(lower[t][:, 256:512], t, 256, 512)
-        cast(2, 0, 128, nc.vector.tensor_copy)
-        cast(2, 128, 256, nc.scalar.copy)
-        nc.scalar.copy(scores[0][:, 256:640], middle[:, 0:384])
-        nc.scalar.copy(scores[1][:, 0:BANK], lower[1][:])
-        cast(3, 0, 128, nc.vector.tensor_copy)
-        quantise_book(2, 0, 256)
-        quantise_book(3, 0, 128)
-        score(early[:, 0:128], 0, 640, 768)
-        score(third_part[:, 0:128], 0, 768, 896)
-        score(last[:, 0:128], 0, 896, C)
-        pat_grouped = keep.tile([P, M, PACK], BF16, tag="book_grouped3", align_bytes=64)
+        scores = {t: keep.tile([P, C], F32, name="scores%d" % t) for t in (0, 1, 3)}
+        first_part = {t: bank("first_part%d" % t, t, LOAD) for t in (0, 1, 3)}
+        lower = bank("lower", 2, BANK)
+        second_part = {t: bank("second_part%d" % t, 4 + t, LOAD) for t in (0, 1)}
+        middle = bank("middle", 6, BANK)
+
+        cast(0, 160, nc.vector.tensor_copy)
+        cast(160, 256, nc.scalar.copy)
+        quantise_book(0, 256)
+        for t in (0, 1, 3):
+            score(t, 0, 256, first_part[t][:])
+        score(2, 0, 256, lower[:, 0:256])
+        cast(256, 384, nc.vector.tensor_copy)
+        cast(384, 512, nc.scalar.copy)
+        quantise_book(256, 512)
+        for t in (0, 1, 3):
+            nc.scalar.copy(scores[t][:, 0:256], first_part[t][:])
+        for t in (0, 1):
+            score(t, 256, 512, second_part[t][:])
+        score(2, 256, 512, lower[:, 256:512])
+        score(3, 256, 512, middle[:, 0:256])
+        cast(512, 640, nc.vector.tensor_copy)
+        cast(640, 768, nc.vector.tensor_copy)
+        quantise_book(512, 640)
+        for t in (0, 1):
+            nc.scalar.copy(scores[t][:, 256:512], second_part[t][:])
+        cast(768, 896, nc.vector.tensor_copy)
+        cast(896, C, nc.vector.tensor_copy)
+        quantise_book(640, 768)
+        quantise_book(768, 896)
+        quantise_book(896, C)
+        third_part, last_part = bank("third_part", 0, LOAD), bank("last_part", 7, LOAD)
+        score(0, 512, 768, third_part[:])
+        score(0, 768, 896, last_part[:, 0:128])
+        score(0, 896, C, last_part[:, 128:256])
+        pat_grouped = keep.tile([P, M, PACK], BF16, tag="book_grouped", align_bytes=64)
         interleave(nc.vector.tensor_copy, pat_grouped[:], pat_raw[:])
-        nc.scalar.copy(scores[0][:, 640:768], early[:, 0:128])
-        nc.vector.tensor_copy(scores[0][:, 768:896], third_part[:, 0:128])
-        nc.scalar.copy(scores[0][:, 896:C], last[:, 0:128])
+        nc.scalar.copy(scores[0][:, 512:768], third_part[:])
+        nc.vector.tensor_copy(scores[0][:, 768:C], last_part[:])
         pat_codes = keep.tile([P, M], U32, align_bytes=64)
         pat_scales = keep.tile([P, M], U8, align_bytes=64)
         quantise(pat_codes[:], pat_scales[:], pat_grouped[:])
         pat_mx = (pat_codes, pat_scales)
-        scores[2] = keep.tile([P, C], F32, name="scores2", tag="book_grouped3", align_bytes=64)
-        scores[3] = keep.tile([P, C], F32, name="scores3", tag="pat_raw")
-        upper[2] = bank("upper2", 6)
-        upper[3] = bank("upper3", 4)
-        for t in (1, 2, 3):
-            score(upper[t][:], t, BANK, C)
+        scores[2] = keep.tile([P, C], F32, name="scores2")
+        end = bank("end", 1, LOAD)
+        upper = {1: bank("upper1", 3, BANK), 2: bank("upper2", 4, BANK)}
+        score(1, 512, 768, upper[1][:, 0:256])
+        score(1, 768, C, upper[1][:, 256:512])
+        score(2, BANK, C, upper[2][:])
+        score(3, 512, 768, middle[:, 256:512])
+        score(3, 768, C, end[:])
+        nc.scalar.copy(scores[2][:, 0:BANK], lower[:])
         nc.scalar.copy(scores[1][:, BANK:C], upper[1][:])
-        nc.scalar.copy(scores[2][:, 0:BANK], lower[2][:])
         nc.scalar.copy(scores[2][:, BANK:C], upper[2][:])
-        nc.scalar.copy(scores[3][:, 0:BANK], lower[3][:])
-        nc.scalar.copy(scores[3][:, BANK:C], upper[3][:])
+        nc.scalar.copy(scores[3][:, 256:768], middle[:])
+        nc.scalar.copy(scores[3][:, 768:C], end[:])
 
         def look_up(s0, width, t, factors):
             piece = offsets[:, s0 // 16 : (s0 + width) // 16]
             c0 = s0 % (2 * PIECE)
             nc.vector.tensor_tensor(looked[s0 // (2 * PIECE)][:, t, c0 : c0 + width], scores[t][:].indirect(piece), factors, MULT)
 
-        plain = shared.tile([P, 2 * PIECE], F32, offset=512, align_bytes=64)
-        nc.scalar.activation(plain[:], scores[3][:].indirect(offsets[:, 0 : 2 * PIECE // 16]), COPY)
-        nc.scalar.activation(looked[0][:, 3, :], plain[:], COPY, scale=fac_sb[:, 3:4])
+        plain = [keep.tile([P, 2 * PIECE], F32, name="plain%d" % h) for h in (0, 1)]
+        for h in (0, 1):
+            nc.scalar.activation(plain[h][:], scores[3][:].indirect(offsets[:, 16 * h : 16 * (h + 1)]), COPY)
+        for h in (0, 1):
+            nc.scalar.activation(looked[h][:, 3, :], plain[h][:], COPY, scale=fac_sb[:, 3:4])
         for t in (0, 1, 2):
             for h in (0, 1):
                 look_up(2 * PIECE * h, 2 * PIECE, t, fac_low[:, t, :])
-        for k in (2, 3):
-            look_up(PIECE * k, PIECE, 3, fac_high[:, 0, :])
 
         def finish(name, grouped, s0, width, bank, copy):
             codes = keep.tile([P, width], U32, name=name + "_codes", align_bytes=64)
@@ -195,12 +195,12 @@ def tile_attend_adcheads_kernel(tc, query, book, fac, pat, offs, out):
             nc.sync.dma_start(out[:, s0 : s0 + width], result[:])
 
         first = keep.tile([P, 2 * PIECE, PACK], BF16, align_bytes=64)
-        third = shared.tile([P, PIECE, PACK], BF16, offset=0, align_bytes=64)
-        fourth = shared.tile([P, PIECE, PACK], BF16, offset=1024, align_bytes=64)
+        third = keep.tile([P, PIECE, PACK], BF16, align_bytes=64)
+        fourth = keep.tile([P, PIECE, PACK], BF16, align_bytes=64)
         interleave(nc.scalar.copy, first[:, 0:PIECE, :], looked[0][:, :, 0:PIECE])
-        interleave(nc.scalar.copy, third[:], looked[1][:, :, 0:PIECE])
         interleave(nc.vector.tensor_copy, first[:, PIECE : 2 * PIECE, :], looked[0][:, :, PIECE : 2 * PIECE])
+        interleave(nc.scalar.copy, third[:], looked[1][:, :, 0:PIECE])
         interleave(nc.vector.tensor_copy, fourth[:], looked[1][:, :, PIECE : 2 * PIECE])
         finish("first", first[:], 0, 2 * PIECE, 7, nc.scalar.copy)
         finish("fourth", fourth[:], 3 * PIECE, PIECE, 0, nc.scalar.copy)
-        finish("third", third[:], 2 * PIECE, PIECE, 1, nc.vector.tensor_copy)
+        finish("third", third[:], 2 * PIECE, PIECE, 2, nc.vector.tensor_copy)

@@ -19,7 +19,9 @@ P = 128
 PACK = 4
 QUAD = 32
 BANK = 512
+HALF = 256
 PIECE = 128
+SHARE = 64
 LOAD = 256
 BOOK_LOADS = (LOAD,) * 4
 
@@ -73,12 +75,13 @@ def tile_attend_adcheads_kernel(tc, query, book, fac, pat, offs, out):
         offsets = keep.tile([P, I // 16], U16)
         nc.sync.dma_start(offsets[:], offs)
 
-        def spread(wide, t0, t1):
-            nc.scalar.copy(wide, fac_sb[:, t0:t1].unsqueeze(2).to_broadcast([P, t1 - t0, wide.shape[2]]))
+        def spread(copy, t):
+            copy(fac_wide[t][:], fac_sb[:, t : t + 1].to_broadcast([P, fac_wide[t].shape[1]]))
 
-        looked = [keep.tile([P, PACK, 2 * PIECE], F32, name="looked%d" % h, tag="looked%d" % h, align_bytes=64) for h in range(2)]
-        fac_low = keep.tile([P, 3, 2 * PIECE], F32)
-        spread(fac_low[:, 0:1, :], 0, 1)
+        looked = keep.tile([P, PACK, I], F32)
+        fac_wide = [keep.tile([P, width], F32, name="fac_wide%d" % t) for t, width in enumerate((I, I, HALF))]
+        spread(nc.scalar.copy, 2)
+        spread(nc.vector.tensor_copy, 0)
 
         q_grouped = keep.tile([P, PACK, P, PACK], BF16, align_bytes=64)
         nc.vector.memset(q_grouped[:], 0.0)
@@ -89,7 +92,7 @@ def tile_attend_adcheads_kernel(tc, query, book, fac, pat, offs, out):
                 q_grouped[parts, :, parts, :].rearrange("p t m j -> p m j t"),
                 q_raw[parts, :, :].rearrange("p j (m t) -> p m j t", t=PACK),
             )
-        spread(fac_low[:, 1:3, :], 1, 3)
+        spread(nc.scalar.copy, 1)
         q_codes = keep.tile([P, Q], U32, align_bytes=64)
         q_scales = keep.tile([P, Q], U8, align_bytes=64)
         quantise(q_codes[:], q_scales[:], q_grouped[:].rearrange("p t m j -> p (t m) j"))
@@ -144,45 +147,46 @@ def tile_attend_adcheads_kernel(tc, query, book, fac, pat, offs, out):
         quantise_book(640, 768)
         quantise_book(768, 896)
         quantise_book(896, C)
-        third_part, last_part = bank("third_part", 0, LOAD), bank("last_part", 7, LOAD)
+        third_part, fourth_part, last_part = bank("third_part", 0, LOAD), bank("fourth_part", 5, PIECE), bank("last_part", 7, PIECE)
         score(0, 512, 768, third_part[:])
-        score(0, 768, 896, last_part[:, 0:128])
-        score(0, 896, C, last_part[:, 128:256])
+        score(0, 768, 896, fourth_part[:])
+        score(0, 896, C, last_part[:])
         pat_grouped = keep.tile([P, M, PACK], BF16, tag="book_grouped", align_bytes=64)
         interleave(nc.vector.tensor_copy, pat_grouped[:], pat_raw[:])
         nc.scalar.copy(scores[0][:, 512:768], third_part[:])
-        nc.vector.tensor_copy(scores[0][:, 768:C], last_part[:])
+        nc.vector.tensor_copy(scores[0][:, 768:896], fourth_part[:])
+        nc.scalar.copy(scores[0][:, 896:C], last_part[:])
         pat_codes = keep.tile([P, M], U32, align_bytes=64)
         pat_scales = keep.tile([P, M], U8, align_bytes=64)
         quantise(pat_codes[:], pat_scales[:], pat_grouped[:])
         pat_mx = (pat_codes, pat_scales)
         scores[2] = keep.tile([P, C], F32, name="scores2")
-        end = bank("end", 1, LOAD)
+        end = bank("end", 5, LOAD)
         upper = {1: bank("upper1", 3, BANK), 2: bank("upper2", 4, BANK)}
         score(1, 512, 768, upper[1][:, 0:256])
         score(1, 768, C, upper[1][:, 256:512])
         score(2, BANK, C, upper[2][:])
-        score(3, 512, 768, middle[:, 256:512])
-        score(3, 768, C, end[:])
+        score(3, 512, 768, end[:])
+        score(3, 768, C, middle[:, 256:512])
         nc.scalar.copy(scores[2][:, 0:BANK], lower[:])
         nc.scalar.copy(scores[1][:, BANK:C], upper[1][:])
         nc.scalar.copy(scores[2][:, BANK:C], upper[2][:])
-        nc.scalar.copy(scores[3][:, 256:768], middle[:])
-        nc.scalar.copy(scores[3][:, 768:C], end[:])
+        nc.scalar.copy(scores[3][:, 512:768], end[:])
+        nc.scalar.copy(scores[3][:].rearrange("p (a c) -> p a c", c=LOAD)[:, 1:4:2, :], middle[:].rearrange("p (a c) -> p a c", c=LOAD))
 
-        def look_up(s0, width, t, factors):
-            piece = offsets[:, s0 // 16 : (s0 + width) // 16]
-            c0 = s0 % (2 * PIECE)
-            nc.vector.tensor_tensor(looked[s0 // (2 * PIECE)][:, t, c0 : c0 + width], scores[t][:].indirect(piece), factors, MULT)
+        def look_up(t, s0, s1):
+            piece = offsets[:, s0 // 16 : s1 // 16]
+            nc.vector.tensor_tensor(looked[:, t, s0:s1], scores[t][:].indirect(piece), fac_wide[t][:, 0 : s1 - s0], MULT)
 
-        plain = [keep.tile([P, 2 * PIECE], F32, name="plain%d" % h) for h in (0, 1)]
-        for h in (0, 1):
-            nc.scalar.activation(plain[h][:], scores[3][:].indirect(offsets[:, 16 * h : 16 * (h + 1)]), COPY)
-        for h in (0, 1):
-            nc.scalar.activation(looked[h][:, 3, :], plain[h][:], COPY, scale=fac_sb[:, 3:4])
-        for t in (0, 1, 2):
-            for h in (0, 1):
-                look_up(2 * PIECE * h, 2 * PIECE, t, fac_low[:, t, :])
+        plain = keep.tile([P, I], F32)
+        for s0 in (0, HALF):
+            nc.scalar.activation(plain[:, s0 : s0 + HALF], scores[3][:].indirect(offsets[:, s0 // 16 : (s0 + HALF) // 16]), COPY)
+        for s0 in (0, HALF):
+            nc.scalar.activation(looked[:, 3, s0 : s0 + HALF], plain[:, s0 : s0 + HALF], COPY, scale=fac_sb[:, 3:4])
+        look_up(0, 0, I)
+        look_up(1, 0, I)
+        look_up(2, 0, HALF)
+        look_up(2, HALF, I)
 
         def finish(name, grouped, s0, width, bank, copy):
             codes = keep.tile([P, width], U32, name=name + "_codes", align_bytes=64)
@@ -194,13 +198,13 @@ def tile_attend_adcheads_kernel(tc, query, book, fac, pat, offs, out):
             copy(result[:], acc[:])
             nc.sync.dma_start(out[:, s0 : s0 + width], result[:])
 
-        first = keep.tile([P, 2 * PIECE, PACK], BF16, align_bytes=64)
+        first = keep.tile([P, HALF, PACK], BF16, align_bytes=64)
         third = keep.tile([P, PIECE, PACK], BF16, align_bytes=64)
         fourth = keep.tile([P, PIECE, PACK], BF16, align_bytes=64)
-        interleave(nc.scalar.copy, first[:, 0:PIECE, :], looked[0][:, :, 0:PIECE])
-        interleave(nc.vector.tensor_copy, first[:, PIECE : 2 * PIECE, :], looked[0][:, :, PIECE : 2 * PIECE])
-        interleave(nc.scalar.copy, third[:], looked[1][:, :, 0:PIECE])
-        interleave(nc.vector.tensor_copy, fourth[:], looked[1][:, :, PIECE : 2 * PIECE])
-        finish("first", first[:], 0, 2 * PIECE, 7, nc.scalar.copy)
-        finish("fourth", fourth[:], 3 * PIECE, PIECE, 0, nc.scalar.copy)
-        finish("third", third[:], 2 * PIECE, PIECE, 2, nc.vector.tensor_copy)
+        interleave(nc.scalar.copy, first[:, 0:SHARE, :], looked[:, :, 0:SHARE])
+        interleave(nc.vector.tensor_copy, first[:, SHARE:HALF, :], looked[:, :, SHARE:HALF])
+        interleave(nc.scalar.copy, third[:], looked[:, :, HALF : HALF + PIECE])
+        interleave(nc.vector.tensor_copy, fourth[:], looked[:, :, HALF + PIECE : I])
+        finish("first", first[:], 0, HALF, 7, nc.scalar.copy)
+        finish("fourth", fourth[:], HALF + PIECE, PIECE, 0, nc.scalar.copy)
+        finish("third", third[:], HALF, PIECE, 2, nc.vector.tensor_copy)

@@ -21,7 +21,7 @@ QUAD = 32
 BANK = 512
 HALF = 256
 PIECE = 128
-SHARE = 64
+SHARE = 96
 LOAD = 256
 BOOK_LOADS = (LOAD,) * 4
 
@@ -101,7 +101,7 @@ def tile_attend_adcheads_kernel(tc, query, book, fac, pat, offs, out):
         book_codes = keep.tile([P, C], U32, align_bytes=64)
         book_scales = keep.tile([P, C], U8, align_bytes=64)
         book_mx = (book_codes, book_scales)
-        book_grouped = keep.tile([P, C, PACK], BF16, tag="book_grouped", align_bytes=64)
+        book_grouped = keep.tile([P, C, PACK], BF16, align_bytes=64)
 
         def cast(c0, c1, copy):
             n, at = divmod(c0, LOAD)
@@ -122,15 +122,17 @@ def tile_attend_adcheads_kernel(tc, query, book, fac, pat, offs, out):
         second_part = {t: bank("second_part%d" % t, 4 + t, LOAD) for t in (0, 1)}
         middle = bank("middle", 6, BANK)
 
-        cast(0, 160, nc.vector.tensor_copy)
-        cast(160, 256, nc.scalar.copy)
+        cast(0, 128, nc.vector.tensor_copy)
+        cast(128, 256, nc.scalar.copy)
         quantise_book(0, 256)
         for t in (0, 1, 3):
             score(t, 0, 256, first_part[t][:])
         score(2, 0, 256, lower[:, 0:256])
         cast(256, 384, nc.vector.tensor_copy)
-        cast(384, 512, nc.scalar.copy)
-        quantise_book(256, 512)
+        cast(384, 416, nc.vector.tensor_copy)
+        cast(416, 512, nc.scalar.copy)
+        quantise_book(256, 384)
+        quantise_book(384, 512)
         for t in (0, 1, 3):
             nc.scalar.copy(scores[t][:, 0:256], first_part[t][:])
         for t in (0, 1):
@@ -151,7 +153,7 @@ def tile_attend_adcheads_kernel(tc, query, book, fac, pat, offs, out):
         score(0, 512, 768, third_part[:])
         score(0, 768, 896, fourth_part[:])
         score(0, 896, C, last_part[:])
-        pat_grouped = keep.tile([P, M, PACK], BF16, tag="book_grouped", align_bytes=64)
+        pat_grouped = keep.tile([P, M, PACK], BF16, tag="book_raw3", align_bytes=64)
         interleave(nc.vector.tensor_copy, pat_grouped[:], pat_raw[:])
         nc.scalar.copy(scores[0][:, 512:768], third_part[:])
         nc.vector.tensor_copy(scores[0][:, 768:896], fourth_part[:])
@@ -162,15 +164,16 @@ def tile_attend_adcheads_kernel(tc, query, book, fac, pat, offs, out):
         pat_mx = (pat_codes, pat_scales)
         scores[2] = keep.tile([P, C], F32, name="scores2")
         end = bank("end", 5, LOAD)
-        upper = {1: bank("upper1", 3, BANK), 2: bank("upper2", 4, BANK)}
-        score(1, 512, 768, upper[1][:, 0:256])
-        score(1, 768, C, upper[1][:, 256:512])
-        score(2, BANK, C, upper[2][:])
+        third1, last1, upper2 = bank("third1", 1, LOAD), bank("last1", 3, LOAD), bank("upper2", 4, BANK)
+        score(1, 512, 768, third1[:])
+        score(1, 768, C, last1[:])
+        score(2, BANK, C, upper2[:])
         score(3, 512, 768, end[:])
         score(3, 768, C, middle[:, 256:512])
         nc.scalar.copy(scores[2][:, 0:BANK], lower[:])
-        nc.scalar.copy(scores[1][:, BANK:C], upper[1][:])
-        nc.scalar.copy(scores[2][:, BANK:C], upper[2][:])
+        nc.scalar.copy(scores[1][:, 512:768], third1[:])
+        nc.scalar.copy(scores[1][:, 768:C], last1[:])
+        nc.scalar.copy(scores[2][:, BANK:C], upper2[:])
         nc.scalar.copy(scores[3][:, 512:768], end[:])
         nc.scalar.copy(scores[3][:].rearrange("p (a c) -> p a c", c=LOAD)[:, 1:4:2, :], middle[:].rearrange("p (a c) -> p a c", c=LOAD))
 
@@ -188,15 +191,11 @@ def tile_attend_adcheads_kernel(tc, query, book, fac, pat, offs, out):
         look_up(2, 0, HALF)
         look_up(2, HALF, I)
 
-        def finish(name, grouped, s0, width, bank, copy):
-            codes = keep.tile([P, width], U32, name=name + "_codes", align_bytes=64)
-            scales = keep.tile([P, width], U8, name=name + "_scales", align_bytes=64)
+        def multiply(name, grouped, acc):
+            codes = keep.tile([P, PIECE], U32, name=name + "_codes", align_bytes=64)
+            scales = keep.tile([P, PIECE], U8, name=name + "_scales", align_bytes=64)
             quantise(codes[:], scales[:], grouped)
-            acc = psum.tile([P, width], F32, name=name + "_acc", tag="bank%d" % bank)
-            product(acc[:], pat_mx, slice(0, M), (codes, scales), slice(0, width))
-            result = keep.tile([P, width], F32, name=name + "_result")
-            copy(result[:], acc[:])
-            nc.sync.dma_start(out[:, s0 : s0 + width], result[:])
+            product(acc, pat_mx, slice(0, M), (codes, scales), slice(0, PIECE))
 
         first = keep.tile([P, HALF, PACK], BF16, align_bytes=64)
         third = keep.tile([P, PIECE, PACK], BF16, align_bytes=64)
@@ -205,6 +204,14 @@ def tile_attend_adcheads_kernel(tc, query, book, fac, pat, offs, out):
         interleave(nc.vector.tensor_copy, first[:, SHARE:HALF, :], looked[:, :, SHARE:HALF])
         interleave(nc.scalar.copy, third[:], looked[:, :, HALF : HALF + PIECE])
         interleave(nc.vector.tensor_copy, fourth[:], looked[:, :, HALF + PIECE : I])
-        finish("first", first[:], 0, HALF, 7, nc.scalar.copy)
-        finish("fourth", fourth[:], HALF + PIECE, PIECE, 0, nc.scalar.copy)
-        finish("third", third[:], HALF, PIECE, 2, nc.vector.tensor_copy)
+        first_acc, third_acc, fourth_acc = bank("first_acc", 7, HALF), bank("third_acc", 2, PIECE), bank("fourth_acc", 0, PIECE)
+        multiply("second", first[:, PIECE:HALF, :], first_acc[:, PIECE:HALF])
+        multiply("first", first[:, 0:PIECE, :], first_acc[:, 0:PIECE])
+        multiply("fourth", fourth[:], fourth_acc[:])
+        multiply("third", third[:], third_acc[:])
+        result = keep.tile([P, I], F32)
+        nc.scalar.copy(result[:, 0:HALF], first_acc[:])
+        nc.sync.dma_start(out[:, 0:HALF], result[:, 0:HALF])
+        nc.scalar.copy(result[:, HALF + PIECE : I], fourth_acc[:])
+        nc.vector.tensor_copy(result[:, HALF : HALF + PIECE], third_acc[:])
+        nc.sync.dma_start(out[:, HALF:I], result[:, HALF:I])

@@ -116,18 +116,17 @@ def tile_attend_adcheads_kernel(tc, query, book, fac, pat, offs, out):
         def bank(name, number, width):
             return psum.tile([P, width], F32, name=name, tag="bank%d" % number)
 
-        scores = {t: keep.tile([P, C], F32, name="scores%d" % t) for t in (0, 1, 3)}
+        scores = [keep.tile([P, C], F32, name="scores%d" % t) for t in range(PACK)]
         first_part = {t: bank("first_part%d" % t, t, LOAD) for t in (0, 1, 3)}
-        lower = bank("lower", 2, BANK)
-        second_part = {t: bank("second_part%d" % t, 4 + t, LOAD) for t in (0, 1)}
-        middle = bank("middle", 6, BANK)
+        lower2 = bank("lower2", 2, BANK)
+        second_part = {0: bank("second_part0", 4, LOAD), 1: bank("second_part1", 5, LOAD), 3: bank("second_part3", 6, LOAD)}
 
         cast(0, 128, nc.vector.tensor_copy)
         cast(128, 256, nc.scalar.copy)
         quantise_book(0, 256)
         for t in (0, 1, 3):
             score(t, 0, 256, first_part[t][:])
-        score(2, 0, 256, lower[:, 0:256])
+        score(2, 0, 256, lower2[:, 0:256])
         cast(256, 384, nc.vector.tensor_copy)
         cast(384, 416, nc.vector.tensor_copy)
         cast(416, 512, nc.scalar.copy)
@@ -135,21 +134,20 @@ def tile_attend_adcheads_kernel(tc, query, book, fac, pat, offs, out):
         quantise_book(384, 512)
         for t in (0, 1, 3):
             nc.scalar.copy(scores[t][:, 0:256], first_part[t][:])
-        for t in (0, 1):
+        for t in (0, 1, 3):
             score(t, 256, 512, second_part[t][:])
-        score(2, 256, 512, lower[:, 256:512])
-        score(3, 256, 512, middle[:, 0:256])
+        score(2, 256, 512, lower2[:, 256:512])
         cast(512, 640, nc.vector.tensor_copy)
         cast(640, 768, nc.vector.tensor_copy)
         quantise_book(512, 640)
-        for t in (0, 1):
+        for t in (0, 1, 3):
             nc.scalar.copy(scores[t][:, 256:512], second_part[t][:])
         cast(768, 896, nc.vector.tensor_copy)
         cast(896, C, nc.vector.tensor_copy)
         quantise_book(640, 768)
         quantise_book(768, 896)
         quantise_book(896, C)
-        third_part, fourth_part, last_part = bank("third_part", 0, LOAD), bank("fourth_part", 5, PIECE), bank("last_part", 7, PIECE)
+        third_part, fourth_part, last_part = bank("third_part", 0, LOAD), bank("fourth_part", 1, PIECE), bank("last_part", 7, PIECE)
         score(0, 512, 768, third_part[:])
         score(0, 768, 896, fourth_part[:])
         score(0, 896, C, last_part[:])
@@ -162,20 +160,14 @@ def tile_attend_adcheads_kernel(tc, query, book, fac, pat, offs, out):
         pat_scales = keep.tile([P, M], U8, align_bytes=64)
         quantise(pat_codes[:], pat_scales[:], pat_grouped[:])
         pat_mx = (pat_codes, pat_scales)
-        scores[2] = keep.tile([P, C], F32, name="scores2")
-        end = bank("end", 5, LOAD)
-        third1, last1, upper2 = bank("third1", 1, LOAD), bank("last1", 3, LOAD), bank("upper2", 4, BANK)
-        score(1, 512, 768, third1[:])
-        score(1, 768, C, last1[:])
-        score(2, BANK, C, upper2[:])
-        score(3, 512, 768, end[:])
-        score(3, 768, C, middle[:, 256:512])
-        nc.scalar.copy(scores[2][:, 0:BANK], lower[:])
-        nc.scalar.copy(scores[1][:, 512:768], third1[:])
-        nc.scalar.copy(scores[1][:, 768:C], last1[:])
-        nc.scalar.copy(scores[2][:, BANK:C], upper2[:])
-        nc.scalar.copy(scores[3][:, 512:768], end[:])
-        nc.scalar.copy(scores[3][:].rearrange("p (a c) -> p a c", c=LOAD)[:, 1:4:2, :], middle[:].rearrange("p (a c) -> p a c", c=LOAD))
+        upper = {t: bank("upper%d" % t, 2 + t, BANK) for t in (1, 2, 3)}
+        score(1, 512, 768, upper[1][:, 0:256])
+        score(1, 768, C, upper[1][:, 256:512])
+        for t in (2, 3):
+            score(t, BANK, C, upper[t][:])
+        nc.scalar.copy(scores[2][:, 0:BANK], lower2[:])
+        for t in (1, 2, 3):
+            nc.scalar.copy(scores[t][:, BANK:C], upper[t][:])
 
         def look_up(t, s0, s1):
             piece = offsets[:, s0 // 16 : s1 // 16]

@@ -205,5 +205,6 @@ def tile_attend_adcheads_kernel(tc, query, book, fac, pat, offs, out):
         nc.scalar.copy(result[:, 0:HALF], first_acc[:])
         nc.sync.dma_start(out[:, 0:HALF], result[:, 0:HALF])
         nc.scalar.copy(result[:, HALF + PIECE : I], fourth_acc[:])
+        nc.sync.dma_start(out[:, HALF + PIECE : I], result[:, HALF + PIECE : I])
         nc.vector.tensor_copy(result[:, HALF : HALF + PIECE], third_acc[:])
-        nc.sync.dma_start(out[:, HALF:I], result[:, HALF:I])
+        nc.sync.dma_start(out[:, HALF : HALF + PIECE], result[:, HALF : HALF + PIECE])

@@ -8,6 +8,7 @@ BYTES = 4 * (4 * 128 * 128 + D * C + Q + Q * M + M * I) + 2 * 128 * (I // 16)
 
 F32 = mybir.dt.float32
 BF16 = mybir.dt.bfloat16
+I32 = mybir.dt.int32
 U32 = mybir.dt.uint32
 U16 = mybir.dt.uint16
 U8 = mybir.dt.uint8
@@ -18,12 +19,10 @@ COPY = mybir.ActivationFunctionType.Copy
 P = 128
 PACK = 4
 QUAD = 32
-BANK = 512
+LOAD = 256
 HALF = 256
 PIECE = 128
-SHARE = 96
-LOAD = 256
-BOOK_LOADS = (LOAD,) * 4
+SHARE = 32
 
 
 def interleave(engine_copy, grouped, planes):
@@ -53,9 +52,12 @@ def tile_attend_adcheads_kernel(tc, query, book, fac, pat, offs, out):
                 stop=True,
             )
 
+        def bank(name, number, width):
+            return psum.tile([P, width], F32, name=name, tag="bank%d" % number)
+
         fac_sb = keep.tile([P, PACK], F32)
         nc.sync.dma_start(fac_sb[:], fac.rearrange("(p t) o -> p (t o)", t=PACK))
-        q_raw = keep.tile([P, PACK, P], F32)
+        q_raw = keep.tile([P, PACK, P], F32, tag="rounded1", align_bytes=64)
         for quad in (0, 2, 1, 3):
             queue = nc.scalar if quad >= 2 else nc.sync
             rows = slice(P * quad, P * (quad + 1))
@@ -64,147 +66,150 @@ def tile_attend_adcheads_kernel(tc, query, book, fac, pat, offs, out):
                 query[rows, rows].rearrange("(p j) c -> p j c", j=PACK),
             )
         book_rows = book.rearrange("(p j) c -> p j c", j=PACK)
-        starts = [sum(BOOK_LOADS[:n]) for n in range(len(BOOK_LOADS))]
         book_raw = []
-        for n, width in enumerate(BOOK_LOADS):
-            raw = keep.tile([P, PACK, width], F32, name="book_raw%d" % n, tag="book_raw%d" % n, align_bytes=64)
-            nc.sync.dma_start(raw[:], book_rows[:, :, starts[n] : starts[n] + width])
+        for n in range(C // LOAD):
+            raw = keep.tile([P, PACK, LOAD], F32, name="book_raw%d" % n, tag="book_raw%d" % n, align_bytes=64)
+            nc.sync.dma_start(raw[:], book_rows[:, :, LOAD * n : LOAD * (n + 1)])
             book_raw.append(raw)
-        pat_raw = keep.tile([P, PACK, M], F32, tag="pat_raw")
+        pat_raw = keep.tile([P, PACK, M], F32)
         nc.sync.dma_start(pat_raw[:], pat.rearrange("(p j) m -> p j m", j=PACK))
         offsets = keep.tile([P, I // 16], U16)
         nc.sync.dma_start(offsets[:], offs)
 
-        def spread(copy, t):
-            copy(fac_wide[t][:], fac_sb[:, t : t + 1].to_broadcast([P, fac_wide[t].shape[1]]))
-
-        looked = keep.tile([P, PACK, I], F32)
-        fac_wide = [keep.tile([P, width], F32, name="fac_wide%d" % t) for t, width in enumerate((I, I, HALF))]
-        spread(nc.scalar.copy, 2)
-        spread(nc.vector.tensor_copy, 0)
-
-        q_grouped = keep.tile([P, PACK, P, PACK], BF16, align_bytes=64)
-        nc.vector.memset(q_grouped[:], 0.0)
-        for quad in (0, 2, 3, 1):
-            parts = slice(QUAD * quad, QUAD * (quad + 1))
-            copy = nc.scalar.copy if quad == 2 else nc.vector.tensor_copy
-            copy(
-                q_grouped[parts, :, parts, :].rearrange("p t m j -> p m j t"),
-                q_raw[parts, :, :].rearrange("p j (m t) -> p m j t", t=PACK),
-            )
-        spread(nc.scalar.copy, 1)
+        zeros = keep.tile([P, Q // 2, PACK], BF16, align_bytes=64)
+        nc.vector.memset(zeros[:], 0.0)
+        square_scales = keep.tile([P, P], U8, align_bytes=64)
+        nc.vector.memset(square_scales[:], 0)
         q_codes = keep.tile([P, Q], U32, align_bytes=64)
         q_scales = keep.tile([P, Q], U8, align_bytes=64)
-        quantise(q_codes[:], q_scales[:], q_grouped[:].rearrange("p t m j -> p (t m) j"))
+        for c0 in (0, Q // 2):
+            quantise(q_codes[:, c0 : c0 + Q // 2], q_scales[:, c0 : c0 + Q // 2], zeros[:])
         q_mx = (q_codes, q_scales)
+
+        fac_wide = [keep.tile([P, width], F32, name="fac_wide%d" % t, tag="fac_wide%d" % t, align_bytes=64) for t, width in enumerate((I, I))]
+
+        def spread(copy, t, s0, s1):
+            copy(fac_wide[t][:, s0:s1], fac_sb[:, t : t + 1].to_broadcast([P, s1 - s0]))
+
+        spread(nc.scalar.copy, 1, 0, I)
+        spread(nc.vector.tensor_copy, 0, 0, I)
+
+        square = keep.tile([P, PACK, QUAD, PACK], BF16, tag="rounded0", align_bytes=64)
+        for copy, m0 in ((nc.vector.tensor_copy, 0), (nc.scalar.copy, QUAD // 2)):
+            copy(
+                square[:, :, m0 : m0 + QUAD // 2, :].rearrange("p t m j -> p m j t"),
+                q_raw[:, :, PACK * m0 : PACK * (m0 + QUAD // 2)].rearrange("p j (m t) -> p m j t", t=PACK),
+            )
+        square_codes = keep.tile([P, P], U32, tag="fac_wide2", align_bytes=64)
+        quantise(square_codes[:], square_scales[:], square[:].rearrange("p t m j -> p (t m) j"))
+        for quad in range(4):
+            parts = slice(QUAD * quad, QUAD * (quad + 1))
+            nc.scalar.copy(
+                q_codes[parts, :].rearrange("p (t m) -> p t m", t=PACK)[:, :, parts],
+                square_codes[parts, :].rearrange("p (t m) -> p t m", t=PACK),
+            )
+        fac_wide.append(keep.tile([P, HALF], F32, name="fac_wide2", tag="fac_wide2", align_bytes=64))
+        spread(nc.scalar.copy, 2, 0, HALF)
+        nc.vector.tensor_copy(
+            q_scales[:].bitcast(I32).rearrange("p (t g w) -> p t g w", t=PACK, g=4),
+            square_scales[:].bitcast(I32).rearrange("p (t w) -> p t w", t=PACK).unsqueeze(2).to_broadcast([P, PACK, 4, QUAD // 4]),
+        )
 
         book_codes = keep.tile([P, C], U32, align_bytes=64)
         book_scales = keep.tile([P, C], U8, align_bytes=64)
         book_mx = (book_codes, book_scales)
-        book_grouped = keep.tile([P, C, PACK], BF16, align_bytes=64)
+        scores = [keep.tile([P, C], F32, name="scores%d" % t) for t in range(PACK)]
 
-        def cast(c0, c1, copy):
-            n, at = divmod(c0, LOAD)
-            interleave(copy, book_grouped[:, c0:c1, :], book_raw[n][:, :, at : at + c1 - c0])
-
-        def quantise_book(c0, c1):
-            quantise(book_codes[:, c0:c1], book_scales[:, c0:c1], book_grouped[:, c0:c1, :])
+        def prepare(n):
+            rounded = [keep.tile([P, PIECE, PACK], BF16, name="rounded%d" % (2 * n + u), tag="rounded%d" % (2 * n + u), align_bytes=64) for u in range(2)]
+            for u in range(2):
+                interleave(nc.vector.tensor_copy, rounded[u][:], book_raw[n][:, :, PIECE * u : PIECE * (u + 1)])
+            for u in range(2):
+                cols = slice(LOAD * n + PIECE * u, LOAD * n + PIECE * (u + 1))
+                quantise(book_codes[:, cols], book_scales[:, cols], rounded[u][:])
 
         def score(t, c0, c1, acc):
             product(acc, q_mx, slice(P * t, P * (t + 1)), book_mx, slice(c0, c1))
 
-        def bank(name, number, width):
-            return psum.tile([P, width], F32, name=name, tag="bank%d" % number)
+        def drained(parts, banks):
+            accs = [bank("early%d_%d" % (t, c0), number, c1 - c0) for (t, c0, c1), number in zip(parts, banks)]
+            for (t, c0, c1), acc in zip(parts, accs):
+                score(t, c0, c1, acc[:])
+            for (t, c0, c1), acc in zip(parts, accs):
+                nc.scalar.copy(scores[t][:, c0:c1], acc[:])
 
-        scores = [keep.tile([P, C], F32, name="scores%d" % t) for t in range(PACK)]
-        first_part = {t: bank("first_part%d" % t, t, LOAD) for t in (0, 1, 3)}
-        lower2 = bank("lower2", 2, BANK)
-        second_part = {0: bank("second_part0", 4, LOAD), 1: bank("second_part1", 5, LOAD), 3: bank("second_part3", 6, LOAD)}
-
-        cast(0, 128, nc.vector.tensor_copy)
-        cast(128, 256, nc.scalar.copy)
-        quantise_book(0, 256)
-        for t in (0, 1, 3):
-            score(t, 0, 256, first_part[t][:])
-        score(2, 0, 256, lower2[:, 0:256])
-        cast(256, 384, nc.vector.tensor_copy)
-        cast(384, 416, nc.vector.tensor_copy)
-        cast(416, 512, nc.scalar.copy)
-        quantise_book(256, 384)
-        quantise_book(384, 512)
-        for t in (0, 1, 3):
-            nc.scalar.copy(scores[t][:, 0:256], first_part[t][:])
-        for t in (0, 1, 3):
-            score(t, 256, 512, second_part[t][:])
-        score(2, 256, 512, lower2[:, 256:512])
-        cast(512, 640, nc.vector.tensor_copy)
-        cast(640, 768, nc.vector.tensor_copy)
-        quantise_book(512, 640)
-        for t in (0, 1, 3):
-            nc.scalar.copy(scores[t][:, 256:512], second_part[t][:])
-        cast(768, 896, nc.vector.tensor_copy)
-        cast(896, C, nc.vector.tensor_copy)
-        quantise_book(640, 768)
-        quantise_book(768, 896)
-        quantise_book(896, C)
-        third_part, fourth_part, last_part = bank("third_part", 0, LOAD), bank("fourth_part", 1, PIECE), bank("last_part", 7, PIECE)
-        score(0, 512, 768, third_part[:])
-        score(0, 768, 896, fourth_part[:])
-        score(0, 896, C, last_part[:])
+        prepare(0)
+        drained([(0, 0, 128), (1, 0, 128), (2, 0, 256), (3, 0, 256), (0, 128, 256), (1, 128, 256)], range(6))
+        prepare(1)
+        drained([(t, 256, 512) for t in range(PACK)], (6, 7, 0, 1))
+        prepare(2)
+        third = {t: bank("third%d" % t, 2 + t, 2 * LOAD if t >= 2 else LOAD) for t in range(PACK)}
+        for t in range(3):
+            score(t, 512, 768, third[t][:, 0:LOAD])
+        for t in (0, 1):
+            nc.scalar.copy(scores[t][:, 512:768], third[t][:])
+        prepare(3)
+        last0 = [bank("last0a", 6, PIECE), bank("last0b", 7, PIECE)]
+        score(0, 768, 896, last0[0][:])
+        score(0, 896, C, last0[1][:])
+        last1 = bank("last1", 0, LOAD)
+        score(1, 768, C, last1[:])
+        score(2, 768, C, third[2][:, LOAD : 2 * LOAD])
+        score(3, 512, C, third[3][:])
         pat_grouped = keep.tile([P, M, PACK], BF16, tag="book_raw3", align_bytes=64)
         interleave(nc.vector.tensor_copy, pat_grouped[:], pat_raw[:])
-        nc.scalar.copy(scores[0][:, 512:768], third_part[:])
-        nc.vector.tensor_copy(scores[0][:, 768:896], fourth_part[:])
-        nc.scalar.copy(scores[0][:, 896:C], last_part[:])
+        nc.vector.tensor_copy(scores[0][:, 768:896], last0[0][:])
+        nc.scalar.copy(scores[0][:, 896:C], last0[1][:])
         pat_codes = keep.tile([P, M], U32, align_bytes=64)
         pat_scales = keep.tile([P, M], U8, align_bytes=64)
         quantise(pat_codes[:], pat_scales[:], pat_grouped[:])
         pat_mx = (pat_codes, pat_scales)
-        upper = {t: bank("upper%d" % t, 2 + t, BANK) for t in (1, 2, 3)}
-        score(1, 512, 768, upper[1][:, 0:256])
-        score(1, 768, C, upper[1][:, 256:512])
-        for t in (2, 3):
-            score(t, BANK, C, upper[t][:])
-        nc.scalar.copy(scores[2][:, 0:BANK], lower2[:])
-        for t in (1, 2, 3):
-            nc.scalar.copy(scores[t][:, BANK:C], upper[t][:])
+        nc.scalar.copy(scores[1][:, 768:C], last1[:])
+        nc.scalar.copy(scores[2][:, 512:C], third[2][:])
+        nc.scalar.copy(scores[3][:, 512:C], third[3][:])
 
-        def look_up(t, s0, s1):
-            piece = offsets[:, s0 // 16 : s1 // 16]
-            nc.vector.tensor_tensor(looked[:, t, s0:s1], scores[t][:].indirect(piece), fac_wide[t][:, 0 : s1 - s0], MULT)
-
+        looked = keep.tile([P, PACK, I], F32)
         plain = keep.tile([P, I], F32)
         for s0 in (0, HALF):
             nc.scalar.activation(plain[:, s0 : s0 + HALF], scores[3][:].indirect(offsets[:, s0 // 16 : (s0 + HALF) // 16]), COPY)
         for s0 in (0, HALF):
             nc.scalar.activation(looked[:, 3, s0 : s0 + HALF], plain[:, s0 : s0 + HALF], COPY, scale=fac_sb[:, 3:4])
+
+        def look_up(t, s0, s1):
+            piece = offsets[:, s0 // 16 : s1 // 16]
+            nc.vector.tensor_tensor(looked[:, t, s0:s1], scores[t][:].indirect(piece), fac_wide[t][:, 0 : s1 - s0], MULT)
+
         look_up(0, 0, I)
         look_up(1, 0, I)
         look_up(2, 0, HALF)
         look_up(2, HALF, I)
 
-        def multiply(name, grouped, acc):
-            codes = keep.tile([P, PIECE], U32, name=name + "_codes", align_bytes=64)
-            scales = keep.tile([P, PIECE], U8, name=name + "_scales", align_bytes=64)
-            quantise(codes[:], scales[:], grouped)
+        grouped = [keep.tile([P, PIECE, PACK], BF16, name="grouped%d" % n, align_bytes=64) for n in range(4)]
+        result = keep.tile([P, I], F32)
+
+        def weave(n, copy, s0=0, s1=PIECE):
+            interleave(copy, grouped[n][:, s0:s1, :], looked[:, :, PIECE * n + s0 : PIECE * n + s1])
+
+        def multiply(n, acc):
+            codes = keep.tile([P, PIECE], U32, name="codes%d" % n, align_bytes=64)
+            scales = keep.tile([P, PIECE], U8, name="scales%d" % n, align_bytes=64)
+            quantise(codes[:], scales[:], grouped[n][:])
             product(acc, pat_mx, slice(0, M), (codes, scales), slice(0, PIECE))
 
-        first = keep.tile([P, HALF, PACK], BF16, align_bytes=64)
-        third = keep.tile([P, PIECE, PACK], BF16, align_bytes=64)
-        fourth = keep.tile([P, PIECE, PACK], BF16, align_bytes=64)
-        interleave(nc.scalar.copy, first[:, 0:SHARE, :], looked[:, :, 0:SHARE])
-        interleave(nc.vector.tensor_copy, first[:, SHARE:HALF, :], looked[:, :, SHARE:HALF])
-        interleave(nc.scalar.copy, third[:], looked[:, :, HALF : HALF + PIECE])
-        interleave(nc.vector.tensor_copy, fourth[:], looked[:, :, HALF + PIECE : I])
-        first_acc, third_acc, fourth_acc = bank("first_acc", 7, HALF), bank("third_acc", 2, PIECE), bank("fourth_acc", 0, PIECE)
-        multiply("second", first[:, PIECE:HALF, :], first_acc[:, PIECE:HALF])
-        multiply("first", first[:, 0:PIECE, :], first_acc[:, 0:PIECE])
-        multiply("fourth", fourth[:], fourth_acc[:])
-        multiply("third", third[:], third_acc[:])
-        result = keep.tile([P, I], F32)
-        nc.scalar.copy(result[:, 0:HALF], first_acc[:])
-        nc.sync.dma_start(out[:, 0:HALF], result[:, 0:HALF])
-        nc.scalar.copy(result[:, HALF + PIECE : I], fourth_acc[:])
-        nc.sync.dma_start(out[:, HALF + PIECE : I], result[:, HALF + PIECE : I])
-        nc.vector.tensor_copy(result[:, HALF : HALF + PIECE], third_acc[:])
-        nc.sync.dma_start(out[:, HALF : HALF + PIECE], result[:, HALF : HALF + PIECE])
+        weave(1, nc.scalar.copy, 0, SHARE)
+        weave(0, nc.scalar.copy)
+        weave(1, nc.vector.tensor_copy, SHARE, PIECE)
+        weave(3, nc.scalar.copy)
+        weave(2, nc.vector.tensor_copy)
+        middle_acc, first_acc, last_acc = bank("middle_acc", 1, HALF), bank("first_acc", 2, PIECE), bank("last_acc", 3, PIECE)
+        multiply(1, middle_acc[:, 0:PIECE])
+        multiply(2, middle_acc[:, PIECE:HALF])
+        multiply(0, first_acc[:])
+        multiply(3, last_acc[:])
+        for copy, acc, s0, s1 in (
+            (nc.scalar.copy, middle_acc, PIECE, PIECE + HALF),
+            (nc.scalar.copy, first_acc, 0, PIECE),
+            (nc.vector.tensor_copy, last_acc, I - PIECE, I),
+        ):
+            copy(result[:, s0:s1], acc[:])
+            nc.sync.dma_start(out[:, s0:s1], result[:, s0:s1])

@@ -22,7 +22,7 @@ QUAD = 32
 LOAD = 256
 HALF = 256
 PIECE = 128
-SHARE = 32
+SHARE = 64
 
 
 def interleave(engine_copy, grouped, planes):
@@ -120,12 +120,17 @@ def tile_attend_adcheads_kernel(tc, query, book, fac, pat, offs, out):
         book_mx = (book_codes, book_scales)
         scores = [keep.tile([P, C], F32, name="scores%d" % t) for t in range(PACK)]
 
-        def prepare(n):
-            rounded = [keep.tile([P, PIECE, PACK], BF16, name="rounded%d" % (2 * n + u), tag="rounded%d" % (2 * n + u), align_bytes=64) for u in range(2)]
-            for u in range(2):
-                interleave(nc.vector.tensor_copy, rounded[u][:], book_raw[n][:, :, PIECE * u : PIECE * (u + 1)])
-            for u in range(2):
-                cols = slice(LOAD * n + PIECE * u, LOAD * n + PIECE * (u + 1))
+        rounded = [keep.tile([P, PIECE, PACK], BF16, name="rounded%d" % u, tag="rounded%d" % u, align_bytes=64) for u in range(C // PIECE)]
+
+        def cast(copy, c0, c1):
+            (u, at), (n, within) = divmod(c0, PIECE), divmod(c0, LOAD)
+            interleave(copy, rounded[u][:, at : at + c1 - c0, :], book_raw[n][:, :, within : within + c1 - c0])
+
+        def prepare(n, upto):
+            cast(nc.vector.tensor_copy, LOAD * n, LOAD * n + PIECE)
+            cast(nc.vector.tensor_copy, LOAD * n + PIECE, upto)
+            for u in (2 * n, 2 * n + 1):
+                cols = slice(PIECE * u, PIECE * (u + 1))
                 quantise(book_codes[:, cols], book_scales[:, cols], rounded[u][:])
 
         def score(t, c0, c1, acc):
@@ -138,24 +143,26 @@ def tile_attend_adcheads_kernel(tc, query, book, fac, pat, offs, out):
             for (t, c0, c1), acc in zip(parts, accs):
                 nc.scalar.copy(scores[t][:, c0:c1], acc[:])
 
-        prepare(0)
+        cast(nc.scalar.copy, C - SHARE, C)
+        prepare(0, 256)
         drained([(0, 0, 128), (1, 0, 128), (2, 0, 256), (3, 0, 256), (0, 128, 256), (1, 128, 256)], range(6))
-        prepare(1)
-        drained([(t, 256, 512) for t in range(PACK)], (6, 7, 0, 1))
-        prepare(2)
-        third = {t: bank("third%d" % t, 2 + t, 2 * LOAD if t >= 2 else LOAD) for t in range(PACK)}
-        for t in range(3):
-            score(t, 512, 768, third[t][:, 0:LOAD])
-        for t in (0, 1):
-            nc.scalar.copy(scores[t][:, 512:768], third[t][:])
-        prepare(3)
-        last0 = [bank("last0a", 6, PIECE), bank("last0b", 7, PIECE)]
+        prepare(1, 512)
+        drained([(0, 256, 512), (1, 256, 512)], (6, 7))
+        mixed = {t: bank("mixed%d" % t, t - 2, 2 * LOAD) for t in (2, 3)}
+        for t in (2, 3):
+            score(t, 256, 512, mixed[t][:, 0:LOAD])
+        prepare(2, 768)
+        drained([(0, 512, 768)], (2,))
+        score(1, 512, 768, mixed[2][:, LOAD : 2 * LOAD])
+        nc.scalar.copy(scores[1][:, 512:768], mixed[2][:, LOAD : 2 * LOAD])
+        prepare(3, C - SHARE)
+        last0 = [bank("last0a", 3, PIECE), bank("last0b", 6, PIECE)]
         score(0, 768, 896, last0[0][:])
         score(0, 896, C, last0[1][:])
-        last1 = bank("last1", 0, LOAD)
-        score(1, 768, C, last1[:])
-        score(2, 768, C, third[2][:, LOAD : 2 * LOAD])
-        score(3, 512, C, third[3][:])
+        score(1, 768, C, mixed[3][:, LOAD : 2 * LOAD])
+        upper = {t: bank("upper%d" % t, 2 + t, 2 * LOAD) for t in (2, 3)}
+        for t in (2, 3):
+            score(t, 512, C, upper[t][:])
         pat_grouped = keep.tile([P, M, PACK], BF16, tag="book_raw3", align_bytes=64)
         interleave(nc.vector.tensor_copy, pat_grouped[:], pat_raw[:])
         nc.vector.tensor_copy(scores[0][:, 768:896], last0[0][:])
@@ -164,9 +171,11 @@ def tile_attend_adcheads_kernel(tc, query, book, fac, pat, offs, out):
         pat_scales = keep.tile([P, M], U8, align_bytes=64)
         quantise(pat_codes[:], pat_scales[:], pat_grouped[:])
         pat_mx = (pat_codes, pat_scales)
-        nc.scalar.copy(scores[1][:, 768:C], last1[:])
-        nc.scalar.copy(scores[2][:, 512:C], third[2][:])
-        nc.scalar.copy(scores[3][:, 512:C], third[3][:])
+        nc.scalar.copy(scores[1][:, 768:C], mixed[3][:, LOAD : 2 * LOAD])
+        for t in (2, 3):
+            nc.scalar.copy(scores[t][:, 256:512], mixed[t][:, 0:LOAD])
+        for t in (2, 3):
+            nc.scalar.copy(scores[t][:, 512:C], upper[t][:])
 
         looked = keep.tile([P, PACK, I], F32)
         plain = keep.tile([P, I], F32)
@@ -187,8 +196,8 @@ def tile_attend_adcheads_kernel(tc, query, book, fac, pat, offs, out):
         grouped = [keep.tile([P, PIECE, PACK], BF16, name="grouped%d" % n, align_bytes=64) for n in range(4)]
         result = keep.tile([P, I], F32)
 
-        def weave(n, copy, s0=0, s1=PIECE):
-            interleave(copy, grouped[n][:, s0:s1, :], looked[:, :, PIECE * n + s0 : PIECE * n + s1])
+        def weave(n, copy):
+            interleave(copy, grouped[n][:], looked[:, :, PIECE * n : PIECE * (n + 1)])
 
         def multiply(n, acc):
             codes = keep.tile([P, PIECE], U32, name="codes%d" % n, align_bytes=64)
@@ -196,20 +205,15 @@ def tile_attend_adcheads_kernel(tc, query, book, fac, pat, offs, out):
             quantise(codes[:], scales[:], grouped[n][:])
             product(acc, pat_mx, slice(0, M), (codes, scales), slice(0, PIECE))
 
-        weave(1, nc.scalar.copy, 0, SHARE)
         weave(0, nc.scalar.copy)
-        weave(1, nc.vector.tensor_copy, SHARE, PIECE)
+        weave(1, nc.vector.tensor_copy)
         weave(3, nc.scalar.copy)
         weave(2, nc.vector.tensor_copy)
-        middle_acc, first_acc, last_acc = bank("middle_acc", 1, HALF), bank("first_acc", 2, PIECE), bank("last_acc", 3, PIECE)
-        multiply(1, middle_acc[:, 0:PIECE])
-        multiply(2, middle_acc[:, PIECE:HALF])
-        multiply(0, first_acc[:])
-        multiply(3, last_acc[:])
-        for copy, acc, s0, s1 in (
-            (nc.scalar.copy, middle_acc, PIECE, PIECE + HALF),
-            (nc.scalar.copy, first_acc, 0, PIECE),
-            (nc.vector.tensor_copy, last_acc, I - PIECE, I),
-        ):
-            copy(result[:, s0:s1], acc[:])
+        accs = {n: bank("acc%d" % n, n, PIECE) for n in range(4)}
+        for n in (1, 2, 0, 3):
+            multiply(n, accs[n][:])
+        for n in (1, 2, 0, 3):
+            copy = nc.vector.tensor_copy if n == 3 else nc.scalar.copy
+            copy(result[:, PIECE * n : PIECE * (n + 1)], accs[n][:])
+        for s0, s1 in ((PIECE, PIECE + HALF), (0, PIECE), (I - PIECE, I)):
             nc.sync.dma_start(out[:, s0:s1], result[:, s0:s1])

@@ -55,16 +55,16 @@ def tile_attend_adcheads_kernel(tc, query, book, fac, pat, offs, out):
         def bank(name, number, width):
             return psum.tile([P, width], F32, name=name, tag="bank%d" % number)
 
-        fac_sb = keep.tile([P, PACK], F32)
-        nc.sync.dma_start(fac_sb[:], fac.rearrange("(p t) o -> p (t o)", t=PACK))
         q_raw = keep.tile([P, PACK, P], F32, tag="rounded1", align_bytes=64)
         for quad in (0, 2, 1, 3):
-            queue = nc.scalar if quad >= 2 else nc.sync
+            queue = nc.scalar if quad == 2 else nc.sync
             rows = slice(P * quad, P * (quad + 1))
             queue.dma_start(
                 q_raw[QUAD * quad : QUAD * (quad + 1), :, :],
                 query[rows, rows].rearrange("(p j) c -> p j c", j=PACK),
             )
+        fac_sb = keep.tile([P, PACK], F32)
+        nc.scalar.dma_start(fac_sb[:], fac.rearrange("(p t) o -> p (t o)", t=PACK))
         book_rows = book.rearrange("(p j) c -> p j c", j=PACK)
         book_raw = []
         for n in range(C // LOAD):
@@ -79,20 +79,12 @@ def tile_attend_adcheads_kernel(tc, query, book, fac, pat, offs, out):
         zeros = keep.tile([P, Q // 2, PACK], BF16, align_bytes=64)
         nc.vector.memset(zeros[:], 0.0)
         square_scales = keep.tile([P, P], U8, align_bytes=64)
-        nc.vector.memset(square_scales[:], 0)
+        nc.scalar.copy(square_scales[:].bitcast(U32), zeros[:].rearrange("p c j -> p (c j)")[:, 0 : P // 2].bitcast(U32))
         q_codes = keep.tile([P, Q], U32, align_bytes=64)
         q_scales = keep.tile([P, Q], U8, align_bytes=64)
         for c0 in (0, Q // 2):
             quantise(q_codes[:, c0 : c0 + Q // 2], q_scales[:, c0 : c0 + Q // 2], zeros[:])
         q_mx = (q_codes, q_scales)
-
-        fac_wide = [keep.tile([P, width], F32, name="fac_wide%d" % t, tag="fac_wide%d" % t, align_bytes=64) for t, width in enumerate((I, I))]
-
-        def spread(copy, t, s0, s1):
-            copy(fac_wide[t][:, s0:s1], fac_sb[:, t : t + 1].to_broadcast([P, s1 - s0]))
-
-        spread(nc.scalar.copy, 1, 0, I)
-        spread(nc.vector.tensor_copy, 0, 0, I)
 
         square = keep.tile([P, PACK, QUAD, PACK], BF16, tag="rounded0", align_bytes=64)
         for copy, m0 in ((nc.vector.tensor_copy, 0), (nc.scalar.copy, QUAD // 2)):
@@ -100,7 +92,7 @@ def tile_attend_adcheads_kernel(tc, query, book, fac, pat, offs, out):
                 square[:, :, m0 : m0 + QUAD // 2, :].rearrange("p t m j -> p m j t"),
                 q_raw[:, :, PACK * m0 : PACK * (m0 + QUAD // 2)].rearrange("p j (m t) -> p m j t", t=PACK),
             )
-        square_codes = keep.tile([P, P], U32, tag="fac_wide2", align_bytes=64)
+        square_codes = keep.tile([P, P], U32, tag="fac_wide", align_bytes=64)
         quantise(square_codes[:], square_scales[:], square[:].rearrange("p t m j -> p (t m) j"))
         for quad in range(4):
             parts = slice(QUAD * quad, QUAD * (quad + 1))
@@ -108,8 +100,8 @@ def tile_attend_adcheads_kernel(tc, query, book, fac, pat, offs, out):
                 q_codes[parts, :].rearrange("p (t m) -> p t m", t=PACK)[:, :, parts],
                 square_codes[parts, :].rearrange("p (t m) -> p t m", t=PACK),
             )
-        fac_wide.append(keep.tile([P, HALF], F32, name="fac_wide2", tag="fac_wide2", align_bytes=64))
-        spread(nc.scalar.copy, 2, 0, HALF)
+        fac_wide = keep.tile([P, 3, HALF], F32, tag="fac_wide", align_bytes=64)
+        nc.scalar.copy(fac_wide[:], fac_sb[:, 0:3].unsqueeze(2).to_broadcast([P, 3, HALF]))
         nc.vector.tensor_copy(
             q_scales[:].bitcast(I32).rearrange("p (t g w) -> p t g w", t=PACK, g=4),
             square_scales[:].bitcast(I32).rearrange("p (t w) -> p t w", t=PACK).unsqueeze(2).to_broadcast([P, PACK, 4, QUAD // 4]),
@@ -186,12 +178,11 @@ def tile_attend_adcheads_kernel(tc, query, book, fac, pat, offs, out):
 
         def look_up(t, s0, s1):
             piece = offsets[:, s0 // 16 : s1 // 16]
-            nc.vector.tensor_tensor(looked[:, t, s0:s1], scores[t][:].indirect(piece), fac_wide[t][:, 0 : s1 - s0], MULT)
+            nc.vector.tensor_tensor(looked[:, t, s0:s1], scores[t][:].indirect(piece), fac_wide[:, t, :], MULT)
 
-        look_up(0, 0, I)
-        look_up(1, 0, I)
-        look_up(2, 0, HALF)
-        look_up(2, HALF, I)
+        for t in range(3):
+            for s0 in (0, HALF):
+                look_up(t, s0, s0 + HALF)
 
         grouped = [keep.tile([P, PIECE, PACK], BF16, name="grouped%d" % n, align_bytes=64) for n in range(4)]
         result = keep.tile([P, I], F32)

from contextlib import ExitStack

import concourse.mybir as mybir

D, C, Q, I, M = 512, 1024, 512, 512, 128
FLOPS = 2 * D * Q * C + 2 * Q * M * I
BYTES = 4 * (4 * 128 * 128 + D * C + Q + Q * M + M * I) + 2 * 128 * (I // 16)

F32 = mybir.dt.float32
BF16 = mybir.dt.bfloat16
I32 = mybir.dt.int32
U32 = mybir.dt.uint32
U16 = mybir.dt.uint16
U8 = mybir.dt.uint8
FP8X4 = mybir.dt.float8_e4m3fn_x4
MULT = mybir.AluOpType.mult
COPY = mybir.ActivationFunctionType.Copy

P = 128
PACK = 4
QUAD = 32
LOAD = 256
HALF = 256
PIECE = 128
SHARE = 64


def interleave(engine_copy, grouped, planes):
    engine_copy(
        grouped.rearrange("p (c i) j -> p c j i", i=4),
        planes.rearrange("p j (c i) -> p c j i", i=4),
    )


def tile_attend_adcheads_kernel(tc, query, book, fac, pat, offs, out):
    nc = tc.nc
    with ExitStack() as ctx:
        keep = ctx.enter_context(tc.tile_pool(name="keep", bufs=1))
        psum = ctx.enter_context(tc.psum_pool(name="psum", bufs=1))

        def quantise(codes, scales, grouped):
            nc.vector.quantize_mx(out=codes.bitcast(FP8X4), scales=scales, in_=grouped.rearrange("p c j -> p (c j)"))

        def product(acc, lhs, lhs_cols, rhs, rhs_cols):
            nc.tensor.matmul_mx(
                out=acc,
                lhsT=lhs[0][:, lhs_cols].bitcast(FP8X4),
                lhsT_scale=lhs[1][:, lhs_cols],
                rhs=rhs[0][:, rhs_cols].bitcast(FP8X4),
                rhs_scale=rhs[1][:, rhs_cols],
                start=True,
                stop=True,
            )

        def bank(name, number, width):
            return psum.tile([P, width], F32, name=name, tag="bank%d" % number)

        q_raw = keep.tile([P, PACK, P], F32, tag="rounded1", align_bytes=64)
        for quad in (0, 2, 1, 3):
            queue = nc.scalar if quad == 2 else nc.sync
            rows = slice(P * quad, P * (quad + 1))
            queue.dma_start(
                q_raw[QUAD * quad : QUAD * (quad + 1), :, :],
                query[rows, rows].rearrange("(p j) c -> p j c", j=PACK),
            )
        fac_sb = keep.tile([P, PACK], F32)
        nc.scalar.dma_start(fac_sb[:], fac.rearrange("(p t) o -> p (t o)", t=PACK))
        book_rows = book.rearrange("(p j) c -> p j c", j=PACK)
        book_raw = []
        for n in range(C // LOAD):
            raw = keep.tile([P, PACK, LOAD], F32, name="book_raw%d" % n, tag="book_raw%d" % n, align_bytes=64)
            nc.sync.dma_start(raw[:], book_rows[:, :, LOAD * n : LOAD * (n + 1)])
            book_raw.append(raw)
        pat_raw = keep.tile([P, PACK, M], F32)
        nc.sync.dma_start(pat_raw[:], pat.rearrange("(p j) m -> p j m", j=PACK))
        offsets = keep.tile([P, I // 16], U16)
        nc.sync.dma_start(offsets[:], offs)

        zeros = keep.tile([P, Q // 2, PACK], BF16, align_bytes=64)
        nc.vector.memset(zeros[:], 0.0)
        square_scales = keep.tile([P, P], U8, align_bytes=64)
        nc.scalar.copy(square_scales[:].bitcast(U32), zeros[:].rearrange("p c j -> p (c j)")[:, 0 : P // 2].bitcast(U32))
        q_codes = keep.tile([P, Q], U32, align_bytes=64)
        q_scales = keep.tile([P, Q], U8, align_bytes=64)
        for c0 in (0, Q // 2):
            quantise(q_codes[:, c0 : c0 + Q // 2], q_scales[:, c0 : c0 + Q // 2], zeros[:])
        q_mx = (q_codes, q_scales)

        square = keep.tile([P, PACK, QUAD, PACK], BF16, tag="rounded0", align_bytes=64)
        for copy, m0 in ((nc.vector.tensor_copy, 0), (nc.scalar.copy, QUAD // 2)):
            copy(
                square[:, :, m0 : m0 + QUAD // 2, :].rearrange("p t m j -> p m j t"),
                q_raw[:, :, PACK * m0 : PACK * (m0 + QUAD // 2)].rearrange("p j (m t) -> p m j t", t=PACK),
            )
        square_codes = keep.tile([P, P], U32, tag="fac_wide", align_bytes=64)
        quantise(square_codes[:], square_scales[:], square[:].rearrange("p t m j -> p (t m) j"))
        for quad in range(4):
            parts = slice(QUAD * quad, QUAD * (quad + 1))
            nc.scalar.copy(
                q_codes[parts, :].rearrange("p (t m) -> p t m", t=PACK)[:, :, parts],
                square_codes[parts, :].rearrange("p (t m) -> p t m", t=PACK),
            )
        fac_wide = keep.tile([P, 3, HALF], F32, tag="fac_wide", align_bytes=64)
        nc.scalar.copy(fac_wide[:], fac_sb[:, 0:3].unsqueeze(2).to_broadcast([P, 3, HALF]))
        nc.vector.tensor_copy(
            q_scales[:].bitcast(I32).rearrange("p (t g w) -> p t g w", t=PACK, g=4),
            square_scales[:].bitcast(I32).rearrange("p (t w) -> p t w", t=PACK).unsqueeze(2).to_broadcast([P, PACK, 4, QUAD // 4]),
        )

        book_codes = keep.tile([P, C], U32, align_bytes=64)
        book_scales = keep.tile([P, C], U8, align_bytes=64)
        book_mx = (book_codes, book_scales)
        scores = [keep.tile([P, C], F32, name="scores%d" % t) for t in range(PACK)]

        rounded = [keep.tile([P, PIECE, PACK], BF16, name="rounded%d" % u, tag="rounded%d" % u, align_bytes=64) for u in range(C // PIECE)]

        def cast(copy, c0, c1):
            (u, at), (n, within) = divmod(c0, PIECE), divmod(c0, LOAD)
            interleave(copy, rounded[u][:, at : at + c1 - c0, :], book_raw[n][:, :, within : within + c1 - c0])

        def prepare(n, upto):
            cast(nc.vector.tensor_copy, LOAD * n, LOAD * n + PIECE)
            cast(nc.vector.tensor_copy, LOAD * n + PIECE, upto)
            for u in (2 * n, 2 * n + 1):
                cols = slice(PIECE * u, PIECE * (u + 1))
                quantise(book_codes[:, cols], book_scales[:, cols], rounded[u][:])

        def score(t, c0, c1, acc):
            product(acc, q_mx, slice(P * t, P * (t + 1)), book_mx, slice(c0, c1))

        def drained(parts, banks):
            accs = [bank("early%d_%d" % (t, c0), number, c1 - c0) for (t, c0, c1), number in zip(parts, banks)]
            for (t, c0, c1), acc in zip(parts, accs):
                score(t, c0, c1, acc[:])
            for (t, c0, c1), acc in zip(parts, accs):
                nc.scalar.copy(scores[t][:, c0:c1], acc[:])

        cast(nc.scalar.copy, C - SHARE, C)
        prepare(0, 256)
        drained([(0, 0, 128), (1, 0, 128), (2, 0, 256), (3, 0, 256), (0, 128, 256), (1, 128, 256)], range(6))
        prepare(1, 512)
        drained([(0, 256, 512), (1, 256, 512)], (6, 7))
        mixed = {t: bank("mixed%d" % t, t - 2, 2 * LOAD) for t in (2, 3)}
        for t in (2, 3):
            score(t, 256, 512, mixed[t][:, 0:LOAD])
        prepare(2, 768)
        drained([(0, 512, 768)], (2,))
        score(1, 512, 768, mixed[2][:, LOAD : 2 * LOAD])
        nc.scalar.copy(scores[1][:, 512:768], mixed[2][:, LOAD : 2 * LOAD])
        prepare(3, C - SHARE)
        last0 = [bank("last0a", 3, PIECE), bank("last0b", 6, PIECE)]
        score(0, 768, 896, last0[0][:])
        score(0, 896, C, last0[1][:])
        score(1, 768, C, mixed[3][:, LOAD : 2 * LOAD])
        upper = {t: bank("upper%d" % t, 2 + t, 2 * LOAD) for t in (2, 3)}
        for t in (2, 3):
            score(t, 512, C, upper[t][:])
        pat_grouped = keep.tile([P, M, PACK], BF16, tag="book_raw3", align_bytes=64)
        interleave(nc.vector.tensor_copy, pat_grouped[:], pat_raw[:])
        nc.vector.tensor_copy(scores[0][:, 768:896], last0[0][:])
        nc.scalar.copy(scores[0][:, 896:C], last0[1][:])
        pat_codes = keep.tile([P, M], U32, align_bytes=64)
        pat_scales = keep.tile([P, M], U8, align_bytes=64)
        quantise(pat_codes[:], pat_scales[:], pat_grouped[:])
        pat_mx = (pat_codes, pat_scales)
        nc.scalar.copy(scores[1][:, 768:C], mixed[3][:, LOAD : 2 * LOAD])
        for t in (2, 3):
            nc.scalar.copy(scores[t][:, 256:512], mixed[t][:, 0:LOAD])
        for t in (2, 3):
            nc.scalar.copy(scores[t][:, 512:C], upper[t][:])

        looked = keep.tile([P, PACK, I], F32)
        plain = keep.tile([P, I], F32)
        for s0 in (0, HALF):
            nc.scalar.activation(plain[:, s0 : s0 + HALF], scores[3][:].indirect(offsets[:, s0 // 16 : (s0 + HALF) // 16]), COPY)
        for s0 in (0, HALF):
            nc.scalar.activation(looked[:, 3, s0 : s0 + HALF], plain[:, s0 : s0 + HALF], COPY, scale=fac_sb[:, 3:4])

        def look_up(t, s0, s1):
            piece = offsets[:, s0 // 16 : s1 // 16]
            nc.vector.tensor_tensor(looked[:, t, s0:s1], scores[t][:].indirect(piece), fac_wide[:, t, :], MULT)

        for t in range(3):
            for s0 in (0, HALF):
                look_up(t, s0, s0 + HALF)

        grouped = [keep.tile([P, PIECE, PACK], BF16, name="grouped%d" % n, align_bytes=64) for n in range(4)]
        result = keep.tile([P, I], F32)

        def weave(n, copy):
            interleave(copy, grouped[n][:], looked[:, :, PIECE * n : PIECE * (n + 1)])

        def multiply(n, acc):
            codes = keep.tile([P, PIECE], U32, name="codes%d" % n, align_bytes=64)
            scales = keep.tile([P, PIECE], U8, name="scales%d" % n, align_bytes=64)
            quantise(codes[:], scales[:], grouped[n][:])
            product(acc, pat_mx, slice(0, M), (codes, scales), slice(0, PIECE))

        weave(0, nc.scalar.copy)
        weave(1, nc.vector.tensor_copy)
        weave(3, nc.scalar.copy)
        weave(2, nc.vector.tensor_copy)
        accs = {n: bank("acc%d" % n, n, PIECE) for n in range(4)}
        for n in (1, 2, 0, 3):
            multiply(n, accs[n][:])
        for n in (1, 2, 0, 3):
            copy = nc.vector.tensor_copy if n == 3 else nc.scalar.copy
            copy(result[:, PIECE * n : PIECE * (n + 1)], accs[n][:])
        for s0, s1 in ((PIECE, PIECE + HALF), (0, PIECE), (I - PIECE, I)):
            nc.sync.dma_start(out[:, s0:s1], result[:, s0:s1])
